import numpy as np
import ml_dtypes


def mxq(x, axis, fmt="e4m3"):
    dtype, down = {"e4m3": (ml_dtypes.float8_e4m3fn, 7), "e5m2": (ml_dtypes.float8_e5m2, 14)}[fmt]
    v = np.moveaxis(np.asarray(x, np.float32).astype(ml_dtypes.bfloat16).astype(np.float64), axis, -1)
    blocks = v.reshape(v.shape[:-1] + (-1, 32))
    amax = np.abs(blocks).max(-1, keepdims=True)
    byte = np.maximum(np.where(amax > 0, np.frexp(amax)[1] - 1 + 127, 0) - down, 1)
    scale = np.exp2(byte - 127.0)
    codes = (blocks / scale).astype(np.float32).astype(dtype).astype(np.float64)
    return np.moveaxis((codes * scale).reshape(v.shape), -1, axis)


WIDE = False


def mx_kscale(k):
    if not WIDE:
        return np.ones(k)
    levels = np.array([10, -10, 5, -5, 0])
    if k % 512:
        return np.exp2(np.random.permutation(np.resize(levels, k // 32))).repeat(32)
    a = np.empty((k // 512, 16))
    for p in range(k // 512):
        a[p, :8] = np.random.permutation(np.resize(levels, 8))
        for g in range(8):
            far = levels[np.abs(levels - a[p, g]) >= 10]
            a[p, g + 8] = far[np.random.randint(len(far))]
    return np.exp2(a.ravel()).repeat(32)


def f64(x):
    return np.asarray(x).astype(np.float64)


def striped(idx):
    return np.tile(idx.reshape(-1, 16).T, (8, 1)).astype(np.uint16)


def unstriped(offs):
    return offs[:16].T.reshape(-1).astype(np.int64)


def striped8(idx):
    return np.concatenate([x.reshape(-1, 16).T for x in idx]).astype(np.uint16)


def runs(offs, k):
    lists = np.stack([offs[16 * r : 16 * r + 16].T.reshape(-1) for r in range(8)]).astype(np.int64)
    return lists[np.arange(k) % 512 // 64]


def pack_weight(w):
    k, n = w.shape
    w = f64(np.asarray(w, np.float32).astype(ml_dtypes.bfloat16)).reshape(k // 32, 32, n)
    amax = np.abs(w).max(1)
    byte = np.clip(np.where(amax > 0, np.frexp(amax)[1] - 1 + 127 - 7, 1), 1, 254)
    scaled = (w * np.exp2(127.0 - byte)[:, None, :]).reshape(k, n).astype(np.float32)
    words = np.ascontiguousarray(scaled.reshape(k // 512, 128, 4, n).transpose(0, 1, 3, 2)).astype(ml_dtypes.float8_e4m3fn).view(np.uint8)
    return words, np.ascontiguousarray(byte.astype(np.uint8).reshape(k // 512, 16, n))


def unpack_weight(words, scales):
    g, p, n, _ = words.shape
    vals = np.ascontiguousarray(words).view(ml_dtypes.float8_e4m3fn).astype(np.float64) * np.repeat(np.exp2(scales.astype(np.float64) - 127.0), 8, axis=1)[..., None]
    return vals.transpose(0, 1, 3, 2).reshape(g * 512, n)


K, T, S, V, N, U, H = 512, 2048, 512, 1024, 512, 1024, 512


def setup_inputs():
    n = np.random.standard_normal
    s = mx_kscale(K)[:, None]
    u = mx_kscale(H)
    packed_xT = pack_weight(n((K, T)) * s)
    return {
        "x_words": packed_xT[0],
        "x_scales": packed_xT[1],
        "w1": (n((K, H)) / np.sqrt(K) / s * u).astype(np.float32),
        "mem": (n((H, U)) * u[:, None]).astype(np.float32),
        "w2": (n((H, N)) / np.sqrt(H) / u[:, None]).astype(np.float32),
        "offs": striped(np.random.permutation(T)[:S]),
        "slot": striped8(np.stack([np.random.permutation(U)[:S] for _ in range(8)])),
        "rd": striped8(np.random.randint(0, U, (8, V))),
    }


def reference(x_words, x_scales, w1, mem, w2, offs, slot, rd):
    xq = unpack_weight(x_words, x_scales)[:, unstriped(offs)]
    y = mxq(f64(w1), 0, "e4m3").T @ xq
    pg = f64(mem).copy()
    pg[np.arange(H)[:, None], runs(slot, H)] = y
    z = pg[np.arange(H)[:, None], runs(rd, H)]
    return mxq(f64(w2), 0, "e4m3").T @ mxq(z, 0, "e4m3")

@@ -1,0 +1,161 @@
+from contextlib import ExitStack
+
+import concourse.mybir as mybir
+
+K, T, S, V, N, U, H = 512, 2048, 512, 1024, 512, 1024, 512
+FLOPS = 2 * K * H * S + 2 * H * N * V
+
+F32 = mybir.dt.float32
+BF16 = mybir.dt.bfloat16
+I32 = mybir.dt.int32
+U32 = mybir.dt.uint32
+U16 = mybir.dt.uint16
+U8 = mybir.dt.uint8
+FP8X4 = mybir.dt.float8_e4m3fn_x4
+
+P = 128
+PACK = 4
+LANES = 16
+CHUNK = 256
+CHUNKS = V // CHUNK
+BANK = 512
+W1_VECTOR_M = 84
+AHEAD = 3
+
+
+def tile_picked_pageread_none_p_kernel(tc, x_words, x_scales, w1, mem, w2, offs, slot, rd, out):
+    nc = tc.nc
+    with ExitStack() as ctx:
+        keep = ctx.enter_context(tc.tile_pool(name="keep", bufs=1))
+        psum = ctx.enter_context(tc.psum_pool(name="psum", bufs=8))
+
+        offs_sb = keep.tile([P, S // LANES], U16, name="offs_sb")
+        slot_sb = keep.tile([P, S // LANES], U16, name="slot_sb")
+        rd_sb = keep.tile([P, V // LANES], U16, name="rd_sb")
+        words_all = keep.tile([P, T], I32, name="words_all", align_bytes=64)
+        scales_all = keep.tile([P, T], U8, name="scales_all", align_bytes=64)
+        w1_raw = keep.tile([P, PACK, H], F32, name="w1_raw", align_bytes=64)
+        w2_raw = keep.tile([P, PACK, N], F32, name="w2_raw", align_bytes=64)
+        page = [keep.tile([P, U], F32, name="page%d" % t, align_bytes=64) for t in range(PACK)]
+        mem_planes = mem.rearrange("(p t) u -> t p u", t=PACK)
+
+        nc.vector.memset(scales_all[:].bitcast(I32), 0)
+        nc.sync.dma_start(offs_sb[:], offs)
+        for q in range(4):
+            nc.scalar.dma_start(scales_all[32 * q : 32 * q + 4, :].bitcast(I32), x_scales[0, 4 * q : 4 * q + 4, :].bitcast(I32))
+        nc.sync.dma_start(w1_raw[:], w1.rearrange("(p j) c -> p j c", j=PACK))
+        nc.sync.dma_start(words_all[:], x_words[0].rearrange("p c r -> p (c r)").bitcast(I32))
+        nc.sync.dma_start(slot_sb[:], slot)
+        nc.sync.dma_start(page[0][:], mem_planes[0])
+        nc.sync.dma_start(page[1][:], mem_planes[1])
+        nc.sync.dma_start(w2_raw[:], w2.rearrange("(p j) c -> p j c", j=PACK))
+        nc.sync.dma_start(page[2][:], mem_planes[2])
+        nc.sync.dma_start(page[3][:], mem_planes[3])
+        nc.sync.dma_start(rd_sb[:], rd)
+
+        x_scale = keep.tile([P, S], U8, name="x_scale", align_bytes=64)
+        nc.vector.tensor_copy(x_scale[:], scales_all[:].indirect(offs_sb[:]))
+
+        w1_grouped = keep.tile([P, H * PACK], BF16, name="w1_grouped", align_bytes=64)
+        w1_dst = w1_grouped[:].rearrange("p (t m j) -> p m j t", t=PACK, j=PACK)
+        w1_src = w1_raw[:].rearrange("p j (m t) -> p m j t", t=PACK)
+        nc.vector.tensor_copy(w1_dst[:, :W1_VECTOR_M], w1_src[:, :W1_VECTOR_M])
+        nc.scalar.copy(w1_dst[:, W1_VECTOR_M:], w1_src[:, W1_VECTOR_M:])
+        w1_codes = keep.tile([P, H], U32, name="w1_codes", align_bytes=64)
+        w1_scale = keep.tile([P, H], U8, name="w1_scale", align_bytes=64)
+        nc.vector.quantize_mx(out=w1_codes[:].bitcast(FP8X4), scales=w1_scale[:], in_=w1_grouped[:])
+
+        x_codes = keep.tile([P, S], U32, name="x_codes", align_bytes=64)
+        half = S // 2
+        for lo in (0, half):
+            nc.vector.tensor_copy(x_codes[:, lo : lo + half], words_all[:].bitcast(U32).indirect(offs_sb[:, lo // LANES : (lo + half) // LANES]))
+
+        for t in range(PACK):
+            y = keep.tile([P, S], F32, name="y%d" % t, tag="y%d" % t, align_bytes=64)
+            features = slice(t * P, (t + 1) * P)
+            width = half if t == 0 else S
+            for lo in range(0, S, width):
+                tokens = slice(lo, lo + width)
+                bank = psum.tile([P, BANK], F32, name="bank")
+                nc.tensor.matmul_mx(
+                    out=bank[:, :width],
+                    lhsT=w1_codes[:, features].bitcast(FP8X4),
+                    lhsT_scale=w1_scale[:, features],
+                    rhs=x_codes[:, tokens].bitcast(FP8X4),
+                    rhs_scale=x_scale[:, tokens],
+                    start=True,
+                    stop=True,
+                )
+                nc.scalar.copy(y[:, tokens], bank[:, :width])
+                nc.vector.tensor_copy(page[t][:].indirect(slot_sb[:, lo // LANES : (lo + width) // LANES]), y[:, tokens])
+
+        w2_grouped = keep.tile([P, N * PACK], BF16, name="w2_grouped", align_bytes=64)
+        nc.scalar.copy(
+            w2_grouped[:].rearrange("p (c i j) -> p c j i", i=4, j=PACK),
+            w2_raw[:].rearrange("p j (c i) -> p c j i", i=4),
+        )
+        w2_codes = keep.tile([P, N], U32, name="w2_codes", align_bytes=64)
+        w2_scale = keep.tile([P, N], U8, name="w2_scale", align_bytes=64)
+        nc.vector.quantize_mx(out=w2_codes[:].bitcast(FP8X4), scales=w2_scale[:], in_=w2_grouped[:])
+
+        strips = PACK * (CHUNKS + 1) + AHEAD
+        z = keep.tile([P, strips * CHUNK], BF16, name="z", tag="y%d" % (PACK - 1), align_bytes=64)
+        z_codes = keep.tile([P, V], U32, name="z_codes", align_bytes=64)
+        z_scale = keep.tile([P, V], U8, name="z_scale", align_bytes=64)
+        out_rows = out.rearrange("(g p) v -> p g v", p=P)
+
+        def gather(n):
+            c, t = divmod(n, PACK)
+            reads = rd_sb[:, c * CHUNK // LANES : (c + 1) * CHUNK // LANES]
+            nc.vector.tensor_copy(z[:, n * CHUNK : (n + 1) * CHUNK], page[t][:].indirect(reads))
+
+        def grouped(c):
+            first = PACK * (c + 1) + AHEAD
+            return z[:, first * CHUNK : (first + PACK) * CHUNK]
+
+        def interleave(c):
+            planes = z[:, PACK * c * CHUNK : PACK * (c + 1) * CHUNK]
+            dst = grouped(c).rearrange("p (a i t) -> p a t i", i=4, t=PACK)
+            src = planes.rearrange("p (t a i) -> p a t i", i=4, t=PACK)
+            if c == CHUNKS - 1:
+                nc.vector.tensor_copy(dst, src)
+            else:
+                nc.scalar.copy(dst, src)
+
+        def quantize(c):
+            cols = slice(c * CHUNK, (c + 1) * CHUNK)
+            nc.vector.quantize_mx(out=z_codes[:, cols].bitcast(FP8X4), scales=z_scale[:, cols], in_=grouped(c))
+
+        def multiply_and_store(c):
+            cols = slice(c * CHUNK, (c + 1) * CHUNK)
+            for b in range(2):
+                bank = psum.tile([P, BANK], F32, name="bank")
+                for h in range(2):
+                    rows = slice((2 * b + h) * P, (2 * b + h + 1) * P)
+                    nc.tensor.matmul_mx(
+                        out=bank[:, h * CHUNK : (h + 1) * CHUNK],
+                        lhsT=w2_codes[:, rows].bitcast(FP8X4),
+                        lhsT_scale=w2_scale[:, rows],
+                        rhs=z_codes[:, cols].bitcast(FP8X4),
+                        rhs_scale=z_scale[:, cols],
+                        start=True,
+                        stop=True,
+                    )
+                result = keep.tile([P, BANK], F32, name="result%d_%d" % (c, b), align_bytes=64)
+                if c == CHUNKS - 1 and b == 1:
+                    nc.vector.tensor_copy(result[:], bank[:])
+                else:
+                    nc.scalar.copy(result[:], bank[:])
+                nc.sync.dma_start(out_rows[:, 2 * b : 2 * b + 2, cols], result[:].rearrange("p (h v) -> p h v", h=2))
+
+        for n in range(PACK * CHUNKS):
+            c, t = divmod(n, PACK)
+            if t == AHEAD and c > 0:
+                quantize(c - 1)
+            gather(n)
+            if t == PACK - 1:
+                interleave(c)
+                if c > 0:
+                    multiply_and_store(c - 1)
+        quantize(CHUNKS - 1)
+        multiply_and_store(CHUNKS - 1)

@@ -19,8 +19,7 @@ LANES = 16
 CHUNK = 256
 CHUNKS = V // CHUNK
 BANK = 512
-W1_VECTOR_M = 84
-AHEAD = 3
+W1_VECTOR_M = 48
 
 
 def tile_picked_pageread_none_p_kernel(tc, x_words, x_scales, w1, mem, w2, offs, slot, rd, out):
@@ -41,9 +40,9 @@ def tile_picked_pageread_none_p_kernel(tc, x_words, x_scales, w1, mem, w2, offs,
 
         nc.vector.memset(scales_all[:].bitcast(I32), 0)
         nc.sync.dma_start(offs_sb[:], offs)
-        for q in range(4):
-            nc.scalar.dma_start(scales_all[32 * q : 32 * q + 4, :].bitcast(I32), x_scales[0, 4 * q : 4 * q + 4, :].bitcast(I32))
         nc.sync.dma_start(w1_raw[:], w1.rearrange("(p j) c -> p j c", j=PACK))
+        for q in range(4):
+            nc.sync.dma_start(scales_all[32 * q : 32 * q + 4, :].bitcast(I32), x_scales[0, 4 * q : 4 * q + 4, :].bitcast(I32))
         nc.sync.dma_start(words_all[:], x_words[0].rearrange("p c r -> p (c r)").bitcast(I32))
         nc.sync.dma_start(slot_sb[:], slot)
         nc.sync.dma_start(page[0][:], mem_planes[0])
@@ -57,8 +56,8 @@ def tile_picked_pageread_none_p_kernel(tc, x_words, x_scales, w1, mem, w2, offs,
         nc.vector.tensor_copy(x_scale[:], scales_all[:].indirect(offs_sb[:]))
 
         w1_grouped = keep.tile([P, H * PACK], BF16, name="w1_grouped", align_bytes=64)
-        w1_dst = w1_grouped[:].rearrange("p (t m j) -> p m j t", t=PACK, j=PACK)
-        w1_src = w1_raw[:].rearrange("p j (m t) -> p m j t", t=PACK)
+        w1_dst = w1_grouped[:].rearrange("p (t m j) -> p m t j", t=PACK, j=PACK)
+        w1_src = w1_raw[:].rearrange("p j (m t) -> p m t j", t=PACK)
         nc.vector.tensor_copy(w1_dst[:, :W1_VECTOR_M], w1_src[:, :W1_VECTOR_M])
         nc.scalar.copy(w1_dst[:, W1_VECTOR_M:], w1_src[:, W1_VECTOR_M:])
         w1_codes = keep.tile([P, H], U32, name="w1_codes", align_bytes=64)
@@ -98,64 +97,68 @@ def tile_picked_pageread_none_p_kernel(tc, x_words, x_scales, w1, mem, w2, offs,
         w2_scale = keep.tile([P, N], U8, name="w2_scale", align_bytes=64)
         nc.vector.quantize_mx(out=w2_codes[:].bitcast(FP8X4), scales=w2_scale[:], in_=w2_grouped[:])
 
-        strips = PACK * (CHUNKS + 1) + AHEAD
-        z = keep.tile([P, strips * CHUNK], BF16, name="z", tag="y%d" % (PACK - 1), align_bytes=64)
+        planes = keep.tile([P, (2 * PACK - 1) * CHUNK], BF16, name="planes", tag="y%d" % (PACK - 1), align_bytes=64)
+        grouped = [keep.tile([P, PACK * CHUNK], BF16, name="grouped%d" % c, align_bytes=64) for c in range(CHUNKS)]
         z_codes = keep.tile([P, V], U32, name="z_codes", align_bytes=64)
         z_scale = keep.tile([P, V], U8, name="z_scale", align_bytes=64)
         out_rows = out.rearrange("(g p) v -> p g v", p=P)
 
-        def gather(n):
-            c, t = divmod(n, PACK)
+        def first_strip(c):
+            return PACK - 1 if c % 2 == 0 else 0
+
+        def gather(c, t):
+            strip = first_strip(c) + t
             reads = rd_sb[:, c * CHUNK // LANES : (c + 1) * CHUNK // LANES]
-            nc.vector.tensor_copy(z[:, n * CHUNK : (n + 1) * CHUNK], page[t][:].indirect(reads))
+            nc.vector.tensor_copy(planes[:, strip * CHUNK : (strip + 1) * CHUNK], page[t][:].indirect(reads))
 
-        def grouped(c):
-            first = PACK * (c + 1) + AHEAD
-            return z[:, first * CHUNK : (first + PACK) * CHUNK]
+        def interleave(c, lo, width, copy):
+            src = planes[:, first_strip(c) * CHUNK : (first_strip(c) + PACK) * CHUNK].rearrange("p (t v) -> p t v", t=PACK)
+            copy(
+                grouped[c][:, PACK * lo : PACK * (lo + width)].rearrange("p (a i t) -> p a t i", i=4, t=PACK),
+                src[:, :, lo : lo + width].rearrange("p t (a i) -> p a t i", i=4),
+            )
 
-        def interleave(c):
-            planes = z[:, PACK * c * CHUNK : PACK * (c + 1) * CHUNK]
-            dst = grouped(c).rearrange("p (a i t) -> p a t i", i=4, t=PACK)
-            src = planes.rearrange("p (t a i) -> p a t i", i=4, t=PACK)
-            if c == CHUNKS - 1:
-                nc.vector.tensor_copy(dst, src)
-            else:
-                nc.scalar.copy(dst, src)
+        def quantize(c, lo, width):
+            cols = slice(c * CHUNK + lo, c * CHUNK + lo + width)
+            nc.vector.quantize_mx(out=z_codes[:, cols].bitcast(FP8X4), scales=z_scale[:, cols], in_=grouped[c][:, PACK * lo : PACK * (lo + width)])
 
-        def quantize(c):
-            cols = slice(c * CHUNK, (c + 1) * CHUNK)
-            nc.vector.quantize_mx(out=z_codes[:, cols].bitcast(FP8X4), scales=z_scale[:, cols], in_=grouped(c))
+        def multiply_and_store(first_col, width, first_group, groups, copy, queue):
+            cols = slice(first_col, first_col + width)
+            bank = psum.tile([P, BANK], F32, name="bank")
+            for h in range(groups):
+                rows = slice((first_group + h) * P, (first_group + h + 1) * P)
+                nc.tensor.matmul_mx(
+                    out=bank[:, h * width : (h + 1) * width],
+                    lhsT=w2_codes[:, rows].bitcast(FP8X4),
+                    lhsT_scale=w2_scale[:, rows],
+                    rhs=z_codes[:, cols].bitcast(FP8X4),
+                    rhs_scale=z_scale[:, cols],
+                    start=True,
+                    stop=True,
+                )
+            result = keep.tile([P, groups * width], F32, name="result%d_%d" % (first_col, first_group), align_bytes=64)
+            copy(result[:], bank[:, : groups * width])
+            queue.dma_start(out_rows[:, first_group : first_group + groups, cols], result[:].rearrange("p (h v) -> p h v", h=groups))
 
-        def multiply_and_store(c):
-            cols = slice(c * CHUNK, (c + 1) * CHUNK)
-            for b in range(2):
-                bank = psum.tile([P, BANK], F32, name="bank")
-                for h in range(2):
-                    rows = slice((2 * b + h) * P, (2 * b + h + 1) * P)
-                    nc.tensor.matmul_mx(
-                        out=bank[:, h * CHUNK : (h + 1) * CHUNK],
-                        lhsT=w2_codes[:, rows].bitcast(FP8X4),
-                        lhsT_scale=w2_scale[:, rows],
-                        rhs=z_codes[:, cols].bitcast(FP8X4),
-                        rhs_scale=z_scale[:, cols],
-                        start=True,
-                        stop=True,
-                    )
-                result = keep.tile([P, BANK], F32, name="result%d_%d" % (c, b), align_bytes=64)
-                if c == CHUNKS - 1 and b == 1:
-                    nc.vector.tensor_copy(result[:], bank[:])
-                else:
-                    nc.scalar.copy(result[:], bank[:])
-                nc.sync.dma_start(out_rows[:, 2 * b : 2 * b + 2, cols], result[:].rearrange("p (h v) -> p h v", h=2))
-
-        for n in range(PACK * CHUNKS):
-            c, t = divmod(n, PACK)
-            if t == AHEAD and c > 0:
-                quantize(c - 1)
-            gather(n)
-            if t == PACK - 1:
-                interleave(c)
-                if c > 0:
-                    multiply_and_store(c - 1)
-        quantize(CHUNKS - 1)
-        multiply_and_store(CHUNKS - 1)
+        last = CHUNKS - 1
+        for c in range(CHUNKS):
+            shared = PACK - 1 - first_strip(c)
+            for t in range(PACK):
+                if t != shared or c == 0:
+                    gather(c, t)
+            if c > 0:
+                quantize(c - 1, 0, CHUNK)
+                gather(c, shared)
+            if c < last:
+                interleave(c, 0, CHUNK, nc.scalar.copy)
+            if c > 0:
+                for g in (0, 2):
+                    multiply_and_store((c - 1) * CHUNK, CHUNK, g, 2, nc.scalar.copy, nc.sync)
+        piece = CHUNK // 2
+        for lo in (0, piece):
+            interleave(last, lo, piece, nc.vector.tensor_copy)
+        for lo in (0, piece):
+            quantize(last, lo, piece)
+        multiply_and_store(last * CHUNK, piece, 0, 4, nc.scalar.copy, nc.sync)
+        multiply_and_store(last * CHUNK + piece, piece, 0, 2, nc.vector.tensor_copy, nc.sync)
+        multiply_and_store(last * CHUNK + piece, piece, 2, 2, nc.scalar.copy, nc.scalar)

@@ -39,10 +39,10 @@ def tile_picked_pageread_none_p_kernel(tc, x_words, x_scales, w1, mem, w2, offs,
         mem_planes = mem.rearrange("(p t) u -> t p u", t=PACK)
 
         nc.vector.memset(scales_all[:].bitcast(I32), 0)
-        nc.sync.dma_start(offs_sb[:], offs)
         nc.sync.dma_start(w1_raw[:], w1.rearrange("(p j) c -> p j c", j=PACK))
-        for q in range(4):
-            nc.sync.dma_start(scales_all[32 * q : 32 * q + 4, :].bitcast(I32), x_scales[0, 4 * q : 4 * q + 4, :].bitcast(I32))
+        nc.sync.dma_start(offs_sb[:], offs)
+        for r in range(4):
+            nc.sync.dma_start(scales_all[r:P:32, :].bitcast(I32), x_scales[0, r:16:4, :].bitcast(I32))
         nc.sync.dma_start(words_all[:], x_words[0].rearrange("p c r -> p (c r)").bitcast(I32))
         nc.sync.dma_start(slot_sb[:], slot)
         nc.sync.dma_start(page[0][:], mem_planes[0])
@@ -70,11 +70,12 @@ def tile_picked_pageread_none_p_kernel(tc, x_words, x_scales, w1, mem, w2, offs,
             nc.vector.tensor_copy(x_codes[:, lo : lo + half], words_all[:].bitcast(U32).indirect(offs_sb[:, lo // LANES : (lo + half) // LANES]))
 
         for t in range(PACK):
-            y = keep.tile([P, S], F32, name="y%d" % t, tag="y%d" % t, align_bytes=64)
+            y = keep.tile([P, S], F32, name="y%d" % t, align_bytes=64)
             features = slice(t * P, (t + 1) * P)
-            width = half if t == 0 else S
-            for lo in range(0, S, width):
-                tokens = slice(lo, lo + width)
+            products = ((0, P), (P, half), (half, S)) if t == 0 else ((0, S),)
+            for lo, hi in products:
+                tokens = slice(lo, hi)
+                width = hi - lo
                 bank = psum.tile([P, BANK], F32, name="bank")
                 nc.tensor.matmul_mx(
                     out=bank[:, :width],
@@ -86,7 +87,8 @@ def tile_picked_pageread_none_p_kernel(tc, x_words, x_scales, w1, mem, w2, offs,
                     stop=True,
                 )
                 nc.scalar.copy(y[:, tokens], bank[:, :width])
-                nc.vector.tensor_copy(page[t][:].indirect(slot_sb[:, lo // LANES : (lo + width) // LANES]), y[:, tokens])
+            for lo, hi in ((0, P), (P, S)) if t == 0 else ((0, S),):
+                nc.vector.tensor_copy(page[t][:].indirect(slot_sb[:, lo // LANES : hi // LANES]), y[:, lo:hi])
 
         w2_grouped = keep.tile([P, N * PACK], BF16, name="w2_grouped", align_bytes=64)
         nc.scalar.copy(
@@ -97,7 +99,7 @@ def tile_picked_pageread_none_p_kernel(tc, x_words, x_scales, w1, mem, w2, offs,
         w2_scale = keep.tile([P, N], U8, name="w2_scale", align_bytes=64)
         nc.vector.quantize_mx(out=w2_codes[:].bitcast(FP8X4), scales=w2_scale[:], in_=w2_grouped[:])
 
-        planes = keep.tile([P, (2 * PACK - 1) * CHUNK], BF16, name="planes", tag="y%d" % (PACK - 1), align_bytes=64)
+        planes = keep.tile([P, (2 * PACK - 1) * CHUNK], BF16, name="planes", align_bytes=64)
         grouped = [keep.tile([P, PACK * CHUNK], BF16, name="grouped%d" % c, align_bytes=64) for c in range(CHUNKS)]
         z_codes = keep.tile([P, V], U32, name="z_codes", align_bytes=64)
         z_scale = keep.tile([P, V], U8, name="z_scale", align_bytes=64)
@@ -159,6 +161,6 @@ def tile_picked_pageread_none_p_kernel(tc, x_words, x_scales, w1, mem, w2, offs,
             interleave(last, lo, piece, nc.vector.tensor_copy)
         for lo in (0, piece):
             quantize(last, lo, piece)
-        multiply_and_store(last * CHUNK, piece, 0, 4, nc.scalar.copy, nc.sync)
-        multiply_and_store(last * CHUNK + piece, piece, 0, 2, nc.vector.tensor_copy, nc.sync)
-        multiply_and_store(last * CHUNK + piece, piece, 2, 2, nc.scalar.copy, nc.scalar)
+        for lo in (0, piece):
+            multiply_and_store(last * CHUNK + lo, piece, 0, 2, nc.scalar.copy, nc.sync)
+            multiply_and_store(last * CHUNK + lo, piece, 2, 2, nc.vector.tensor_copy, nc.sync)

@@ -44,8 +44,8 @@ def tile_picked_pageread_none_p_kernel(tc, x_words, x_scales, w1, mem, w2, offs,
         for r in range(4):
             nc.sync.dma_start(scales_all[r:P:32, :].bitcast(I32), x_scales[0, r:16:4, :].bitcast(I32))
         nc.sync.dma_start(words_all[:], x_words[0].rearrange("p c r -> p (c r)").bitcast(I32))
-        nc.sync.dma_start(slot_sb[:], slot)
         nc.sync.dma_start(page[0][:], mem_planes[0])
+        nc.sync.dma_start(slot_sb[:], slot)
         nc.sync.dma_start(page[1][:], mem_planes[1])
         nc.sync.dma_start(w2_raw[:], w2.rearrange("(p j) c -> p j c", j=PACK))
         nc.sync.dma_start(page[2][:], mem_planes[2])
@@ -113,12 +113,14 @@ def tile_picked_pageread_none_p_kernel(tc, x_words, x_scales, w1, mem, w2, offs,
             reads = rd_sb[:, c * CHUNK // LANES : (c + 1) * CHUNK // LANES]
             nc.vector.tensor_copy(planes[:, strip * CHUNK : (strip + 1) * CHUNK], page[t][:].indirect(reads))
 
-        def interleave(c, lo, width, copy):
-            src = planes[:, first_strip(c) * CHUNK : (first_strip(c) + PACK) * CHUNK].rearrange("p (t v) -> p t v", t=PACK)
-            copy(
-                grouped[c][:, PACK * lo : PACK * (lo + width)].rearrange("p (a i t) -> p a t i", i=4, t=PACK),
-                src[:, :, lo : lo + width].rearrange("p t (a i) -> p a t i", i=4),
-            )
+        def strips(c):
+            return planes[:, first_strip(c) * CHUNK : (first_strip(c) + PACK) * CHUNK].rearrange("p (t v) -> p v t", t=PACK)
+
+        def interleave(c):
+            nc.gpsimd.tensor_scalar(grouped[c][:].rearrange("p (v t) -> p v t", t=PACK), strips(c), 1.0, 0.0, mybir.AluOpType.mult, mybir.AluOpType.add)
+
+        def weave_pair(c, t, lo, width, copy):
+            copy(grouped[c][:].rearrange("p (v t) -> p v t", t=PACK)[:, lo : lo + width, t : t + 2], strips(c)[:, lo : lo + width, t : t + 2])
 
         def quantize(c, lo, width):
             cols = slice(c * CHUNK + lo, c * CHUNK + lo + width)
@@ -152,13 +154,15 @@ def tile_picked_pageread_none_p_kernel(tc, x_words, x_scales, w1, mem, w2, offs,
                 quantize(c - 1, 0, CHUNK)
                 gather(c, shared)
             if c < last:
-                interleave(c, 0, CHUNK, nc.scalar.copy)
+                interleave(c)
+            else:
+                weave_pair(last, 0, 0, CHUNK, nc.scalar.copy)
             if c > 0:
                 for g in (0, 2):
                     multiply_and_store((c - 1) * CHUNK, CHUNK, g, 2, nc.scalar.copy, nc.sync)
         piece = CHUNK // 2
         for lo in (0, piece):
-            interleave(last, lo, piece, nc.vector.tensor_copy)
+            weave_pair(last, 2, lo, piece, nc.vector.tensor_copy)
         for lo in (0, piece):
             quantize(last, lo, piece)
         for lo in (0, piece):

@@ -12,6 +12,7 @@ U32 = mybir.dt.uint32
 U16 = mybir.dt.uint16
 U8 = mybir.dt.uint8
 FP8X4 = mybir.dt.float8_e4m3fn_x4
+COPY = mybir.ActivationFunctionType.Copy
 
 P = 128
 PACK = 4
@@ -20,6 +21,7 @@ CHUNK = 256
 CHUNKS = V // CHUNK
 BANK = 512
 W1_VECTOR_M = 48
+STRIP_OF_PLANE = (1, 2, 0, 1)
 
 
 def tile_picked_pageread_none_p_kernel(tc, x_words, x_scales, w1, mem, w2, offs, slot, rd, out):
@@ -48,9 +50,9 @@ def tile_picked_pageread_none_p_kernel(tc, x_words, x_scales, w1, mem, w2, offs,
         nc.sync.dma_start(slot_sb[:], slot)
         nc.sync.dma_start(page[1][:], mem_planes[1])
         nc.sync.dma_start(w2_raw[:], w2.rearrange("(p j) c -> p j c", j=PACK))
+        nc.sync.dma_start(rd_sb[:], rd)
         nc.sync.dma_start(page[2][:], mem_planes[2])
         nc.sync.dma_start(page[3][:], mem_planes[3])
-        nc.sync.dma_start(rd_sb[:], rd)
 
         x_scale = keep.tile([P, S], U8, name="x_scale", align_bytes=64)
         nc.vector.tensor_copy(x_scale[:], scales_all[:].indirect(offs_sb[:]))
@@ -90,49 +92,52 @@ def tile_picked_pageread_none_p_kernel(tc, x_words, x_scales, w1, mem, w2, offs,
             for lo, hi in ((0, P), (P, S)) if t == 0 else ((0, S),):
                 nc.vector.tensor_copy(page[t][:].indirect(slot_sb[:, lo // LANES : hi // LANES]), y[:, lo:hi])
 
-        w2_grouped = keep.tile([P, N * PACK], BF16, name="w2_grouped", align_bytes=64)
-        nc.scalar.copy(
-            w2_grouped[:].rearrange("p (c i j) -> p c j i", i=4, j=PACK),
-            w2_raw[:].rearrange("p j (c i) -> p c j i", i=4),
-        )
-        w2_codes = keep.tile([P, N], U32, name="w2_codes", align_bytes=64)
-        w2_scale = keep.tile([P, N], U8, name="w2_scale", align_bytes=64)
-        nc.vector.quantize_mx(out=w2_codes[:].bitcast(FP8X4), scales=w2_scale[:], in_=w2_grouped[:])
-
-        planes = keep.tile([P, (2 * PACK - 1) * CHUNK], BF16, name="planes", align_bytes=64)
+        strips = keep.tile([P, (PACK - 1) * V], BF16, name="strips", align_bytes=64)
         grouped = [keep.tile([P, PACK * CHUNK], BF16, name="grouped%d" % c, align_bytes=64) for c in range(CHUNKS)]
         z_codes = keep.tile([P, V], U32, name="z_codes", align_bytes=64)
         z_scale = keep.tile([P, V], U8, name="z_scale", align_bytes=64)
         out_rows = out.rearrange("(g p) v -> p g v", p=P)
 
-        def first_strip(c):
-            return PACK - 1 if c % 2 == 0 else 0
+        def gather(t, lo, width):
+            first = STRIP_OF_PLANE[t] * V + lo
+            reads = rd_sb[:, lo // LANES : (lo + width) // LANES]
+            nc.scalar.activation(strips[:, first : first + width], page[t][:].indirect(reads), COPY)
 
-        def gather(c, t):
-            strip = first_strip(c) + t
-            reads = rd_sb[:, c * CHUNK // LANES : (c + 1) * CHUNK // LANES]
-            nc.vector.tensor_copy(planes[:, strip * CHUNK : (strip + 1) * CHUNK], page[t][:].indirect(reads))
+        def pair_views(c, t):
+            strip = STRIP_OF_PLANE[t]
+            src = strips[:].rearrange("p (s v) -> p v s", v=V)[:, c * CHUNK : (c + 1) * CHUNK, strip : strip + 2]
+            dst = grouped[c][:].rearrange("p (v t) -> p v t", t=PACK)[:, :, t : t + 2]
+            return dst, src
 
-        def strips(c):
-            return planes[:, first_strip(c) * CHUNK : (first_strip(c) + PACK) * CHUNK].rearrange("p (t v) -> p v t", t=PACK)
+        w2_grouped = keep.tile([P, N * PACK], BF16, name="w2_grouped", align_bytes=64)
+        nc.scalar.copy(
+            w2_grouped[:].rearrange("p (c i j) -> p c j i", i=4, j=PACK),
+            w2_raw[:].rearrange("p j (c i) -> p c j i", i=4),
+        )
+        for t in (0, 1):
+            for lo in (0, V // 2):
+                gather(t, lo, V // 2)
+        for c in range(CHUNKS):
+            dst, src = pair_views(c, 0)
+            nc.gpsimd.tensor_scalar(dst, src, 1.0, 0.0, mybir.AluOpType.mult, mybir.AluOpType.add)
 
-        def interleave(c):
-            nc.gpsimd.tensor_scalar(grouped[c][:].rearrange("p (v t) -> p v t", t=PACK), strips(c), 1.0, 0.0, mybir.AluOpType.mult, mybir.AluOpType.add)
+        for lo in (0, V // 2):
+            gather(2, lo, V // 2)
+        w2_codes = keep.tile([P, N], U32, name="w2_codes", tag="y3", align_bytes=64)
+        w2_scale = keep.tile([P, N], U8, name="w2_scale", align_bytes=64)
+        nc.vector.quantize_mx(out=w2_codes[:].bitcast(FP8X4), scales=w2_scale[:], in_=w2_grouped[:])
 
-        def weave_pair(c, t, lo, width, copy):
-            copy(grouped[c][:].rearrange("p (v t) -> p v t", t=PACK)[:, lo : lo + width, t : t + 2], strips(c)[:, lo : lo + width, t : t + 2])
+        def quantize(c):
+            cols = slice(c * CHUNK, (c + 1) * CHUNK)
+            nc.vector.quantize_mx(out=z_codes[:, cols].bitcast(FP8X4), scales=z_scale[:, cols], in_=grouped[c][:])
 
-        def quantize(c, lo, width):
-            cols = slice(c * CHUNK + lo, c * CHUNK + lo + width)
-            nc.vector.quantize_mx(out=z_codes[:, cols].bitcast(FP8X4), scales=z_scale[:, cols], in_=grouped[c][:, PACK * lo : PACK * (lo + width)])
-
-        def multiply_and_store(first_col, width, first_group, groups, copy, queue):
-            cols = slice(first_col, first_col + width)
+        def multiply_and_store(c, first_group, copy):
+            cols = slice(c * CHUNK, (c + 1) * CHUNK)
             bank = psum.tile([P, BANK], F32, name="bank")
-            for h in range(groups):
+            for h in range(2):
                 rows = slice((first_group + h) * P, (first_group + h + 1) * P)
                 nc.tensor.matmul_mx(
-                    out=bank[:, h * width : (h + 1) * width],
+                    out=bank[:, h * CHUNK : (h + 1) * CHUNK],
                     lhsT=w2_codes[:, rows].bitcast(FP8X4),
                     lhsT_scale=w2_scale[:, rows],
                     rhs=z_codes[:, cols].bitcast(FP8X4),
@@ -140,31 +145,18 @@ def tile_picked_pageread_none_p_kernel(tc, x_words, x_scales, w1, mem, w2, offs,
                     start=True,
                     stop=True,
                 )
-            result = keep.tile([P, groups * width], F32, name="result%d_%d" % (first_col, first_group), align_bytes=64)
-            copy(result[:], bank[:, : groups * width])
-            queue.dma_start(out_rows[:, first_group : first_group + groups, cols], result[:].rearrange("p (h v) -> p h v", h=groups))
+            result = keep.tile([P, BANK], F32, name="result%d_%d" % (c, first_group), align_bytes=64)
+            copy(result[:], bank[:])
+            nc.sync.dma_start(out_rows[:, first_group : first_group + 2, cols], result[:].rearrange("p (h v) -> p h v", h=2))
 
-        last = CHUNKS - 1
         for c in range(CHUNKS):
-            shared = PACK - 1 - first_strip(c)
-            for t in range(PACK):
-                if t != shared or c == 0:
-                    gather(c, t)
+            gather(3, c * CHUNK, CHUNK)
+        for c in range(CHUNKS):
+            nc.vector.tensor_copy(*pair_views(c, 2))
             if c > 0:
-                quantize(c - 1, 0, CHUNK)
-                gather(c, shared)
-            if c < last:
-                interleave(c)
-            else:
-                weave_pair(last, 0, 0, CHUNK, nc.scalar.copy)
-            if c > 0:
-                for g in (0, 2):
-                    multiply_and_store((c - 1) * CHUNK, CHUNK, g, 2, nc.scalar.copy, nc.sync)
-        piece = CHUNK // 2
-        for lo in (0, piece):
-            weave_pair(last, 2, lo, piece, nc.vector.tensor_copy)
-        for lo in (0, piece):
-            quantize(last, lo, piece)
-        for lo in (0, piece):
-            multiply_and_store(last * CHUNK + lo, piece, 0, 2, nc.scalar.copy, nc.sync)
-            multiply_and_store(last * CHUNK + lo, piece, 2, 2, nc.vector.tensor_copy, nc.sync)
+                quantize(c - 1)
+        quantize(CHUNKS - 1)
+        for c in range(CHUNKS):
+            for g in (0, 2):
+                on_vector = c == 2 or (c == 3 and g == 0)
+                multiply_and_store(c, g, nc.vector.tensor_copy if on_vector else nc.scalar.copy)

@@ -98,15 +98,19 @@ def tile_picked_pageread_none_p_kernel(tc, x_words, x_scales, w1, mem, w2, offs,
         z_scale = keep.tile([P, V], U8, name="z_scale", align_bytes=64)
         out_rows = out.rearrange("(g p) v -> p g v", p=P)
 
-        def gather(t, lo, width):
+        def gather_views(t, lo, width):
             first = STRIP_OF_PLANE[t] * V + lo
             reads = rd_sb[:, lo // LANES : (lo + width) // LANES]
-            nc.scalar.activation(strips[:, first : first + width], page[t][:].indirect(reads), COPY)
+            return strips[:, first : first + width], page[t][:].indirect(reads)
 
-        def pair_views(c, t):
+        def gather(t, lo, width):
+            nc.scalar.activation(*gather_views(t, lo, width), COPY)
+
+        def pair_views(c, t, lo=0, width=CHUNK):
             strip = STRIP_OF_PLANE[t]
-            src = strips[:].rearrange("p (s v) -> p v s", v=V)[:, c * CHUNK : (c + 1) * CHUNK, strip : strip + 2]
-            dst = grouped[c][:].rearrange("p (v t) -> p v t", t=PACK)[:, :, t : t + 2]
+            first = c * CHUNK + lo
+            src = strips[:].rearrange("p (s v) -> p v s", v=V)[:, first : first + width, strip : strip + 2]
+            dst = grouped[c][:].rearrange("p (v t) -> p v t", t=PACK)[:, lo : lo + width, t : t + 2]
             return dst, src
 
         w2_grouped = keep.tile([P, N * PACK], BF16, name="w2_grouped", align_bytes=64)
@@ -127,17 +131,20 @@ def tile_picked_pageread_none_p_kernel(tc, x_words, x_scales, w1, mem, w2, offs,
         w2_scale = keep.tile([P, N], U8, name="w2_scale", align_bytes=64)
         nc.vector.quantize_mx(out=w2_codes[:].bitcast(FP8X4), scales=w2_scale[:], in_=w2_grouped[:])
 
-        def quantize(c):
-            cols = slice(c * CHUNK, (c + 1) * CHUNK)
-            nc.vector.quantize_mx(out=z_codes[:, cols].bitcast(FP8X4), scales=z_scale[:, cols], in_=grouped[c][:])
+        def weave(c, lo=0, width=CHUNK):
+            nc.vector.tensor_copy(*pair_views(c, 2, lo, width))
 
-        def multiply_and_store(c, first_group, copy):
-            cols = slice(c * CHUNK, (c + 1) * CHUNK)
+        def quantize(c, lo=0, width=CHUNK):
+            cols = slice(c * CHUNK + lo, c * CHUNK + lo + width)
+            nc.vector.quantize_mx(out=z_codes[:, cols].bitcast(FP8X4), scales=z_scale[:, cols], in_=grouped[c][:, PACK * lo : PACK * (lo + width)])
+
+        def multiply_and_store(first_col, width, first_group, groups, copy):
+            cols = slice(first_col, first_col + width)
             bank = psum.tile([P, BANK], F32, name="bank")
-            for h in range(2):
+            for h in range(groups):
                 rows = slice((first_group + h) * P, (first_group + h + 1) * P)
                 nc.tensor.matmul_mx(
-                    out=bank[:, h * CHUNK : (h + 1) * CHUNK],
+                    out=bank[:, h * width : (h + 1) * width],
                     lhsT=w2_codes[:, rows].bitcast(FP8X4),
                     lhsT_scale=w2_scale[:, rows],
                     rhs=z_codes[:, cols].bitcast(FP8X4),
@@ -145,18 +152,23 @@ def tile_picked_pageread_none_p_kernel(tc, x_words, x_scales, w1, mem, w2, offs,
                     start=True,
                     stop=True,
                 )
-            result = keep.tile([P, BANK], F32, name="result%d_%d" % (c, first_group), align_bytes=64)
-            copy(result[:], bank[:])
-            nc.sync.dma_start(out_rows[:, first_group : first_group + 2, cols], result[:].rearrange("p (h v) -> p h v", h=2))
+            result = keep.tile([P, groups * width], F32, name="result%d_%d" % (first_col, first_group), align_bytes=64)
+            copy(result[:], bank[:, : groups * width])
+            nc.sync.dma_start(out_rows[:, first_group : first_group + groups, cols], result[:].rearrange("p (h v) -> p h v", h=groups))
 
         for c in range(CHUNKS):
             gather(3, c * CHUNK, CHUNK)
-        for c in range(CHUNKS):
-            nc.vector.tensor_copy(*pair_views(c, 2))
-            if c > 0:
-                quantize(c - 1)
-        quantize(CHUNKS - 1)
-        for c in range(CHUNKS):
-            for g in (0, 2):
-                on_vector = c == 2 or (c == 3 and g == 0)
-                multiply_and_store(c, g, nc.vector.tensor_copy if on_vector else nc.scalar.copy)
+        weave(0)
+        quantize(0)
+        weave(1)
+        weave(2)
+        quantize(1)
+        weave(3)
+        quantize(2)
+        quantize(3)
+        for g in range(PACK):
+            multiply_and_store(0, CHUNK, g, 1, nc.scalar.copy)
+        for g in (0, 2):
+            multiply_and_store(CHUNK, CHUNK, g, 2, nc.scalar.copy)
+        for g in range(PACK):
+            multiply_and_store(2 * CHUNK, 2 * CHUNK, g, 1, nc.vector.tensor_copy if g % 2 == 0 else nc.scalar.copy)

@@ -48,9 +48,9 @@ def tile_picked_pageread_none_p_kernel(tc, x_words, x_scales, w1, mem, w2, offs,
         nc.sync.dma_start(words_all[:], x_words[0].rearrange("p c r -> p (c r)").bitcast(I32))
         nc.sync.dma_start(page[0][:], mem_planes[0])
         nc.sync.dma_start(slot_sb[:], slot)
-        nc.sync.dma_start(page[1][:], mem_planes[1])
-        nc.sync.dma_start(w2_raw[:], w2.rearrange("(p j) c -> p j c", j=PACK))
         nc.sync.dma_start(rd_sb[:], rd)
+        nc.sync.dma_start(w2_raw[:], w2.rearrange("(p j) c -> p j c", j=PACK))
+        nc.sync.dma_start(page[1][:], mem_planes[1])
         nc.sync.dma_start(page[2][:], mem_planes[2])
         nc.sync.dma_start(page[3][:], mem_planes[3])
 
@@ -129,7 +129,6 @@ def tile_picked_pageread_none_p_kernel(tc, x_words, x_scales, w1, mem, w2, offs,
             gather(2, lo, V // 2)
         w2_codes = keep.tile([P, N], U32, name="w2_codes", tag="y3", align_bytes=64)
         w2_scale = keep.tile([P, N], U8, name="w2_scale", align_bytes=64)
-        nc.vector.quantize_mx(out=w2_codes[:].bitcast(FP8X4), scales=w2_scale[:], in_=w2_grouped[:])
 
         def weave(c, lo=0, width=CHUNK):
             nc.vector.tensor_copy(*pair_views(c, 2, lo, width))
@@ -138,37 +137,48 @@ def tile_picked_pageread_none_p_kernel(tc, x_words, x_scales, w1, mem, w2, offs,
             cols = slice(c * CHUNK + lo, c * CHUNK + lo + width)
             nc.vector.quantize_mx(out=z_codes[:, cols].bitcast(FP8X4), scales=z_scale[:, cols], in_=grouped[c][:, PACK * lo : PACK * (lo + width)])
 
-        def multiply_and_store(first_col, width, first_group, groups, copy):
+        def multiply_and_store(first_col, width, first_group, groups, copies):
             cols = slice(first_col, first_col + width)
-            bank = psum.tile([P, BANK], F32, name="bank")
-            for h in range(groups):
-                rows = slice((first_group + h) * P, (first_group + h + 1) * P)
-                nc.tensor.matmul_mx(
-                    out=bank[:, h * width : (h + 1) * width],
-                    lhsT=w2_codes[:, rows].bitcast(FP8X4),
-                    lhsT_scale=w2_scale[:, rows],
-                    rhs=z_codes[:, cols].bitcast(FP8X4),
-                    rhs_scale=z_scale[:, cols],
-                    start=True,
-                    stop=True,
-                )
+            per_bank = groups // len(copies)
             result = keep.tile([P, groups * width], F32, name="result%d_%d" % (first_col, first_group), align_bytes=64)
-            copy(result[:], bank[:, : groups * width])
+            for b, copy in enumerate(copies):
+                bank = psum.tile([P, BANK], F32, name="bank")
+                for h in range(per_bank):
+                    group = first_group + b * per_bank + h
+                    rows = slice(group * P, (group + 1) * P)
+                    nc.tensor.matmul_mx(
+                        out=bank[:, h * width : (h + 1) * width],
+                        lhsT=w2_codes[:, rows].bitcast(FP8X4),
+                        lhsT_scale=w2_scale[:, rows],
+                        rhs=z_codes[:, cols].bitcast(FP8X4),
+                        rhs_scale=z_scale[:, cols],
+                        start=True,
+                        stop=True,
+                    )
+                copy(result[:, b * per_bank * width : (b + 1) * per_bank * width], bank[:, : per_bank * width])
             nc.sync.dma_start(out_rows[:, first_group : first_group + groups, cols], result[:].rearrange("p (h v) -> p h v", h=groups))
 
-        for c in range(CHUNKS):
+        def quantize_w2(first_group):
+            rows = slice(first_group * P, (first_group + 2) * P)
+            nc.vector.quantize_mx(out=w2_codes[:, rows].bitcast(FP8X4), scales=w2_scale[:, rows], in_=w2_grouped[:, PACK * rows.start : PACK * rows.stop])
+
+        nc.vector.tensor_copy(*gather_views(3, 0, CHUNK))
+        for c in range(1, CHUNKS):
             gather(3, c * CHUNK, CHUNK)
+        quantize_w2(0)
         weave(0)
+        quantize_w2(2)
         quantize(0)
         weave(1)
         weave(2)
+        nc.scalar.copy(*pair_views(3, 2))
         quantize(1)
-        weave(3)
         quantize(2)
         quantize(3)
+        on_scalar, on_vector = nc.scalar.copy, nc.vector.tensor_copy
         for g in range(PACK):
-            multiply_and_store(0, CHUNK, g, 1, nc.scalar.copy)
+            multiply_and_store(0, CHUNK, g, 1, [on_scalar])
         for g in (0, 2):
-            multiply_and_store(CHUNK, CHUNK, g, 2, nc.scalar.copy)
+            multiply_and_store(CHUNK, CHUNK, g, 2, [on_scalar])
         for g in range(PACK):
-            multiply_and_store(2 * CHUNK, 2 * CHUNK, g, 1, nc.vector.tensor_copy if g % 2 == 0 else nc.scalar.copy)
+            multiply_and_store(2 * CHUNK, 2 * CHUNK, g, 1, [on_vector if g % 2 == 0 else on_scalar])

@@ -158,27 +158,33 @@ def tile_picked_pageread_none_p_kernel(tc, x_words, x_scales, w1, mem, w2, offs,
                 copy(result[:, b * per_bank * width : (b + 1) * per_bank * width], bank[:, : per_bank * width])
             nc.sync.dma_start(out_rows[:, first_group : first_group + groups, cols], result[:].rearrange("p (h v) -> p h v", h=groups))
 
-        def quantize_w2(first_group):
-            rows = slice(first_group * P, (first_group + 2) * P)
+        def quantize_w2(first_group, groups):
+            rows = slice(first_group * P, (first_group + groups) * P)
             nc.vector.quantize_mx(out=w2_codes[:, rows].bitcast(FP8X4), scales=w2_scale[:, rows], in_=w2_grouped[:, PACK * rows.start : PACK * rows.stop])
 
         nc.vector.tensor_copy(*gather_views(3, 0, CHUNK))
         for c in range(1, CHUNKS):
             gather(3, c * CHUNK, CHUNK)
-        quantize_w2(0)
-        weave(0)
-        quantize_w2(2)
-        quantize(0)
+        piece = CHUNK // 2
+        quantize_w2(0, 2)
+        weave(0, 0, piece)
+        weave(0, piece, piece)
+        quantize(0, 0, piece)
+        quantize(0, piece, piece)
+        quantize_w2(2, 1)
+        quantize_w2(3, 1)
         weave(1)
         weave(2)
-        nc.scalar.copy(*pair_views(3, 2))
         quantize(1)
+        weave(3)
         quantize(2)
         quantize(3)
         on_scalar, on_vector = nc.scalar.copy, nc.vector.tensor_copy
-        for g in range(PACK):
-            multiply_and_store(0, CHUNK, g, 1, [on_scalar])
+        multiply_and_store(0, CHUNK, 0, 1, [on_scalar])
+        multiply_and_store(0, CHUNK, 1, 1, [on_scalar])
+        multiply_and_store(0, CHUNK, 2, 2, [on_scalar, on_scalar])
         for g in (0, 2):
-            multiply_and_store(CHUNK, CHUNK, g, 2, [on_scalar])
-        for g in range(PACK):
-            multiply_and_store(2 * CHUNK, 2 * CHUNK, g, 1, [on_vector if g % 2 == 0 else on_scalar])
+            multiply_and_store(CHUNK, CHUNK, g, 2, [on_scalar, on_scalar])
+        multiply_and_store(2 * CHUNK, 2 * CHUNK, 0, 1, [on_vector])
+        multiply_and_store(2 * CHUNK, 2 * CHUNK, 1, 1, [on_scalar])
+        multiply_and_store(2 * CHUNK, 2 * CHUNK, 2, 2, [on_vector, on_scalar])

@@ -114,9 +114,13 @@ def tile_picked_pageread_none_p_kernel(tc, x_words, x_scales, w1, mem, w2, offs,
             return dst, src
 
         w2_grouped = keep.tile([P, N * PACK], BF16, name="w2_grouped", align_bytes=64)
-        nc.scalar.copy(
-            w2_grouped[:].rearrange("p (c i j) -> p c j i", i=4, j=PACK),
-            w2_raw[:].rearrange("p j (c i) -> p c j i", i=4),
+        nc.gpsimd.tensor_scalar(
+            w2_grouped[:].rearrange("p (c j) -> p c j", j=PACK),
+            w2_raw[:].rearrange("p j c -> p c j"),
+            1.0,
+            0.0,
+            mybir.AluOpType.mult,
+            mybir.AluOpType.add,
         )
         for t in (0, 1):
             for lo in (0, V // 2):
@@ -180,11 +184,8 @@ def tile_picked_pageread_none_p_kernel(tc, x_words, x_scales, w1, mem, w2, offs,
         quantize(2)
         quantize(3)
         on_scalar, on_vector = nc.scalar.copy, nc.vector.tensor_copy
-        multiply_and_store(0, CHUNK, 0, 1, [on_scalar])
-        multiply_and_store(0, CHUNK, 1, 1, [on_scalar])
-        multiply_and_store(0, CHUNK, 2, 2, [on_scalar, on_scalar])
-        for g in (0, 2):
-            multiply_and_store(CHUNK, CHUNK, g, 2, [on_scalar, on_scalar])
-        multiply_and_store(2 * CHUNK, 2 * CHUNK, 0, 1, [on_vector])
-        multiply_and_store(2 * CHUNK, 2 * CHUNK, 1, 1, [on_scalar])
-        multiply_and_store(2 * CHUNK, 2 * CHUNK, 2, 2, [on_vector, on_scalar])
+        for c in (0, 1):
+            for g in range(PACK):
+                multiply_and_store(c * CHUNK, CHUNK, g, 1, [on_scalar])
+        for g in range(PACK):
+            multiply_and_store(2 * CHUNK, 2 * CHUNK, g, 1, [on_scalar if g % 2 == 0 else on_vector])

@@ -67,14 +67,14 @@ def tile_picked_pageread_none_p_kernel(tc, x_words, x_scales, w1, mem, w2, offs,
         nc.vector.quantize_mx(out=w1_codes[:].bitcast(FP8X4), scales=w1_scale[:], in_=w1_grouped[:])
 
         x_codes = keep.tile([P, S], U32, name="x_codes", align_bytes=64)
-        half = S // 2
-        for lo in (0, half):
-            nc.vector.tensor_copy(x_codes[:, lo : lo + half], words_all[:].bitcast(U32).indirect(offs_sb[:, lo // LANES : (lo + half) // LANES]))
+        token_pieces = ((0, P), (P, S - P), (S - P, S))
+        for lo, hi in token_pieces:
+            nc.vector.tensor_copy(x_codes[:, lo:hi], words_all[:].bitcast(U32).indirect(offs_sb[:, lo // LANES : hi // LANES]))
 
         for t in range(PACK):
             y = keep.tile([P, S], F32, name="y%d" % t, align_bytes=64)
             features = slice(t * P, (t + 1) * P)
-            products = ((0, P), (P, half), (half, S)) if t == 0 else ((0, S),)
+            products = token_pieces if t == 0 else ((0, S),)
             for lo, hi in products:
                 tokens = slice(lo, hi)
                 width = hi - lo
@@ -141,26 +141,23 @@ def tile_picked_pageread_none_p_kernel(tc, x_words, x_scales, w1, mem, w2, offs,
             cols = slice(c * CHUNK + lo, c * CHUNK + lo + width)
             nc.vector.quantize_mx(out=z_codes[:, cols].bitcast(FP8X4), scales=z_scale[:, cols], in_=grouped[c][:, PACK * lo : PACK * (lo + width)])
 
-        def multiply_and_store(first_col, width, first_group, groups, copies):
+        def multiply(dst, group, first_col, width):
+            rows = slice(group * P, (group + 1) * P)
             cols = slice(first_col, first_col + width)
-            per_bank = groups // len(copies)
-            result = keep.tile([P, groups * width], F32, name="result%d_%d" % (first_col, first_group), align_bytes=64)
-            for b, copy in enumerate(copies):
-                bank = psum.tile([P, BANK], F32, name="bank")
-                for h in range(per_bank):
-                    group = first_group + b * per_bank + h
-                    rows = slice(group * P, (group + 1) * P)
-                    nc.tensor.matmul_mx(
-                        out=bank[:, h * width : (h + 1) * width],
-                        lhsT=w2_codes[:, rows].bitcast(FP8X4),
-                        lhsT_scale=w2_scale[:, rows],
-                        rhs=z_codes[:, cols].bitcast(FP8X4),
-                        rhs_scale=z_scale[:, cols],
-                        start=True,
-                        stop=True,
-                    )
-                copy(result[:, b * per_bank * width : (b + 1) * per_bank * width], bank[:, : per_bank * width])
-            nc.sync.dma_start(out_rows[:, first_group : first_group + groups, cols], result[:].rearrange("p (h v) -> p h v", h=groups))
+            nc.tensor.matmul_mx(
+                out=dst,
+                lhsT=w2_codes[:, rows].bitcast(FP8X4),
+                lhsT_scale=w2_scale[:, rows],
+                rhs=z_codes[:, cols].bitcast(FP8X4),
+                rhs_scale=z_scale[:, cols],
+                start=True,
+                stop=True,
+            )
+
+        def store(bank, group, first_col, width, copy):
+            result = keep.tile([P, width], F32, name="result%d_%d" % (first_col, group), align_bytes=64)
+            copy(result[:], bank[:, :width])
+            nc.sync.dma_start(out_rows[:, group, first_col : first_col + width], result[:])
 
         def quantize_w2(first_group, groups):
             rows = slice(first_group * P, (first_group + groups) * P)
@@ -176,16 +173,24 @@ def tile_picked_pageread_none_p_kernel(tc, x_words, x_scales, w1, mem, w2, offs,
         quantize(0, 0, piece)
         quantize(0, piece, piece)
         quantize_w2(2, 1)
+        weave(1, 0, piece)
+        weave(1, piece, piece)
         quantize_w2(3, 1)
-        weave(1)
+        quantize(1, 0, piece)
+        quantize(1, piece, piece)
         weave(2)
-        quantize(1)
         weave(3)
         quantize(2)
         quantize(3)
-        on_scalar, on_vector = nc.scalar.copy, nc.vector.tensor_copy
         for c in (0, 1):
             for g in range(PACK):
-                multiply_and_store(c * CHUNK, CHUNK, g, 1, [on_scalar])
+                bank = psum.tile([P, BANK], F32, name="bank")
+                multiply(bank[:, :CHUNK], g, c * CHUNK, CHUNK)
+                store(bank, g, c * CHUNK, CHUNK, nc.scalar.copy)
+        wide = [psum.tile([P, BANK], F32, name="bank") for g in range(PACK)]
+        for c in (2, 3):
+            multiply(wide[0][:, (c - 2) * CHUNK : (c - 1) * CHUNK], 0, c * CHUNK, CHUNK)
+        for g in range(1, PACK):
+            multiply(wide[g][:], g, 2 * CHUNK, 2 * CHUNK)
         for g in range(PACK):
-            multiply_and_store(2 * CHUNK, 2 * CHUNK, g, 1, [on_scalar if g % 2 == 0 else on_vector])
+            store(wide[g], g, 2 * CHUNK, 2 * CHUNK, nc.scalar.copy if g % 2 == 0 else nc.vector.tensor_copy)

@@ -51,8 +51,9 @@ def tile_picked_pageread_none_p_kernel(tc, x_words, x_scales, w1, mem, w2, offs,
         nc.sync.dma_start(rd_sb[:], rd)
         nc.sync.dma_start(w2_raw[:], w2.rearrange("(p j) c -> p j c", j=PACK))
         nc.sync.dma_start(page[1][:], mem_planes[1])
-        nc.sync.dma_start(page[2][:], mem_planes[2])
-        nc.sync.dma_start(page[3][:], mem_planes[3])
+        for t in (2, 3):
+            for lo in range(0, U, U // 4):
+                nc.sync.dma_start(page[t][:, lo : lo + U // 4], mem_planes[t][:, lo : lo + U // 4])
 
         x_scale = keep.tile([P, S], U8, name="x_scale", align_bytes=64)
         nc.vector.tensor_copy(x_scale[:], scales_all[:].indirect(offs_sb[:]))
@@ -163,10 +164,11 @@ def tile_picked_pageread_none_p_kernel(tc, x_words, x_scales, w1, mem, w2, offs,
             rows = slice(first_group * P, (first_group + groups) * P)
             nc.vector.quantize_mx(out=w2_codes[:, rows].bitcast(FP8X4), scales=w2_scale[:, rows], in_=w2_grouped[:, PACK * rows.start : PACK * rows.stop])
 
+        piece = CHUNK // 2
         nc.vector.tensor_copy(*gather_views(3, 0, CHUNK))
         for c in range(1, CHUNKS):
             gather(3, c * CHUNK, CHUNK)
-        piece = CHUNK // 2
+        nc.scalar.copy(*pair_views(2, 2, piece, piece))
         quantize_w2(0, 2)
         weave(0, 0, piece)
         weave(0, piece, piece)
@@ -178,7 +180,7 @@ def tile_picked_pageread_none_p_kernel(tc, x_words, x_scales, w1, mem, w2, offs,
         quantize_w2(3, 1)
         quantize(1, 0, piece)
         quantize(1, piece, piece)
-        weave(2)
+        weave(2, 0, piece)
         weave(3)
         quantize(2)
         quantize(3)
@@ -187,10 +189,13 @@ def tile_picked_pageread_none_p_kernel(tc, x_words, x_scales, w1, mem, w2, offs,
                 bank = psum.tile([P, BANK], F32, name="bank")
                 multiply(bank[:, :CHUNK], g, c * CHUNK, CHUNK)
                 store(bank, g, c * CHUNK, CHUNK, nc.scalar.copy)
-        wide = [psum.tile([P, BANK], F32, name="bank") for g in range(PACK)]
+        first_wide = keep.tile([P, 2 * CHUNK], F32, name="first_wide", align_bytes=64)
         for c in (2, 3):
-            multiply(wide[0][:, (c - 2) * CHUNK : (c - 1) * CHUNK], 0, c * CHUNK, CHUNK)
+            bank = psum.tile([P, BANK], F32, name="bank")
+            multiply(bank[:, :CHUNK], 0, c * CHUNK, CHUNK)
+            nc.vector.tensor_copy(first_wide[:, (c - 2) * CHUNK : (c - 1) * CHUNK], bank[:, :CHUNK])
+        nc.sync.dma_start(out_rows[:, 0, 2 * CHUNK :], first_wide[:])
         for g in range(1, PACK):
-            multiply(wide[g][:], g, 2 * CHUNK, 2 * CHUNK)
-        for g in range(PACK):
-            store(wide[g], g, 2 * CHUNK, 2 * CHUNK, nc.scalar.copy if g % 2 == 0 else nc.vector.tensor_copy)
+            bank = psum.tile([P, BANK], F32, name="bank")
+            multiply(bank[:], g, 2 * CHUNK, 2 * CHUNK)
+            store(bank, g, 2 * CHUNK, 2 * CHUNK, nc.vector.tensor_copy if g % 2 == 0 else nc.scalar.copy)

@@ -168,7 +168,7 @@ def tile_picked_pageread_none_p_kernel(tc, x_words, x_scales, w1, mem, w2, offs,
         nc.vector.tensor_copy(*gather_views(3, 0, CHUNK))
         for c in range(1, CHUNKS):
             gather(3, c * CHUNK, CHUNK)
-        nc.scalar.copy(*pair_views(2, 2, piece, piece))
+        nc.scalar.copy(*pair_views(2, 2, 192, 64))
         quantize_w2(0, 2)
         weave(0, 0, piece)
         weave(0, piece, piece)
@@ -180,14 +180,15 @@ def tile_picked_pageread_none_p_kernel(tc, x_words, x_scales, w1, mem, w2, offs,
         quantize_w2(3, 1)
         quantize(1, 0, piece)
         quantize(1, piece, piece)
-        weave(2, 0, piece)
+        weave(2, 0, 192)
         weave(3)
         quantize(2)
         quantize(3)
         for c in (0, 1):
             for g in range(PACK):
                 bank = psum.tile([P, BANK], F32, name="bank")
-                multiply(bank[:, :CHUNK], g, c * CHUNK, CHUNK)
+                for lo, width in ((0, piece), (piece, piece)) if g == 0 else ((0, CHUNK),):
+                    multiply(bank[:, lo : lo + width], g, c * CHUNK + lo, width)
                 store(bank, g, c * CHUNK, CHUNK, nc.scalar.copy)
         first_wide = keep.tile([P, 2 * CHUNK], F32, name="first_wide", align_bytes=64)
         for c in (2, 3):

@@ -13,6 +13,8 @@ U16 = mybir.dt.uint16
 U8 = mybir.dt.uint8
 FP8X4 = mybir.dt.float8_e4m3fn_x4
 COPY = mybir.ActivationFunctionType.Copy
+MULT = mybir.AluOpType.mult
+ADD = mybir.AluOpType.add
 
 P = 128
 PACK = 4
@@ -20,6 +22,7 @@ LANES = 16
 CHUNK = 256
 CHUNKS = V // CHUNK
 BANK = 512
+QUADRANT = 32
 W1_VECTOR_M = 48
 STRIP_OF_PLANE = (1, 2, 0, 1)
 
@@ -27,50 +30,61 @@ STRIP_OF_PLANE = (1, 2, 0, 1)
 def tile_picked_pageread_none_p_kernel(tc, x_words, x_scales, w1, mem, w2, offs, slot, rd, out):
     nc = tc.nc
     with ExitStack() as ctx:
+        lists = ctx.enter_context(tc.tile_pool(name="lists", bufs=1))
         keep = ctx.enter_context(tc.tile_pool(name="keep", bufs=1))
         psum = ctx.enter_context(tc.psum_pool(name="psum", bufs=8))
 
-        offs_sb = keep.tile([P, S // LANES], U16, name="offs_sb")
-        slot_sb = keep.tile([P, S // LANES], U16, name="slot_sb")
-        rd_sb = keep.tile([P, V // LANES], U16, name="rd_sb")
+        offs_sb = lists.tile([P, S // LANES], U16, name="offs_sb")
+        slot_sb = lists.tile([P, S // LANES], U16, name="slot_sb")
+        rd_sb = lists.tile([P, V // LANES], U16, name="rd_sb")
         words_all = keep.tile([P, T], I32, name="words_all", align_bytes=64)
         scales_all = keep.tile([P, T], U8, name="scales_all", align_bytes=64)
         w1_raw = keep.tile([P, PACK, H], F32, name="w1_raw", align_bytes=64)
-        w2_raw = keep.tile([P, PACK, N], F32, name="w2_raw", align_bytes=64)
-        page = [keep.tile([P, U], F32, name="page%d" % t, align_bytes=64) for t in range(PACK)]
+        x_scale = keep.tile([P, S], U8, name="x_scale", align_bytes=64)
+        w1_rows = w1.rearrange("(p j) c -> p j c", j=PACK)
         mem_planes = mem.rearrange("(p t) u -> t p u", t=PACK)
 
         nc.vector.memset(scales_all[:].bitcast(I32), 0)
-        nc.sync.dma_start(w1_raw[:], w1.rearrange("(p j) c -> p j c", j=PACK))
+        nc.vector.memset(x_scale[:].bitcast(I32), 0)
+        nc.sync.dma_start(w1_raw[:, :1], w1_rows[:, :1])
         nc.sync.dma_start(offs_sb[:], offs)
-        for r in range(4):
-            nc.sync.dma_start(scales_all[r:P:32, :].bitcast(I32), x_scales[0, r:16:4, :].bitcast(I32))
+        nc.sync.dma_start(scales_all[32:96:4, :].bitcast(I32), x_scales[0].bitcast(I32))
+        nc.sync.dma_start(w1_raw[:, 1:], w1_rows[:, 1:])
         nc.sync.dma_start(words_all[:], x_words[0].rearrange("p c r -> p (c r)").bitcast(I32))
-        nc.sync.dma_start(page[0][:], mem_planes[0])
         nc.sync.dma_start(slot_sb[:], slot)
         nc.sync.dma_start(rd_sb[:], rd)
-        nc.sync.dma_start(w2_raw[:], w2.rearrange("(p j) c -> p j c", j=PACK))
-        nc.sync.dma_start(page[1][:], mem_planes[1])
-        for t in (2, 3):
-            for lo in range(0, U, U // 4):
-                nc.sync.dma_start(page[t][:, lo : lo + U // 4], mem_planes[t][:, lo : lo + U // 4])
 
-        x_scale = keep.tile([P, S], U8, name="x_scale", align_bytes=64)
-        nc.vector.tensor_copy(x_scale[:], scales_all[:].indirect(offs_sb[:]))
+        picked_scales = keep.tile([P, S], U8, name="picked_scales", align_bytes=64)
+        nc.vector.tensor_copy(picked_scales[:], scales_all[:].indirect(offs_sb[:]))
+        for q in range(4):
+            first = 32 + 16 * q
+            nc.sync.dma_start(x_scale[QUADRANT * q : QUADRANT * q + 4, :].bitcast(I32), picked_scales[first : first + 16 : 4, :].bitcast(I32))
+
+        def load_page(t, after):
+            plane = keep.tile([P, U], F32, name="page%d" % t, tag=after, align_bytes=64)
+            nc.sync.dma_start(plane[:], mem_planes[t])
+            return plane
+
+        page = [load_page(0, "scales_all")]
 
         w1_grouped = keep.tile([P, H * PACK], BF16, name="w1_grouped", align_bytes=64)
         w1_dst = w1_grouped[:].rearrange("p (t m j) -> p m t j", t=PACK, j=PACK)
         w1_src = w1_raw[:].rearrange("p j (m t) -> p m t j", t=PACK)
         nc.vector.tensor_copy(w1_dst[:, :W1_VECTOR_M], w1_src[:, :W1_VECTOR_M])
-        nc.scalar.copy(w1_dst[:, W1_VECTOR_M:], w1_src[:, W1_VECTOR_M:])
+        for rows in (slice(0, 1), slice(1, PACK)):
+            nc.scalar.copy(w1_dst[:, W1_VECTOR_M:, :, rows], w1_src[:, W1_VECTOR_M:, :, rows])
+        page.append(load_page(1, "w1_raw"))
         w1_codes = keep.tile([P, H], U32, name="w1_codes", align_bytes=64)
         w1_scale = keep.tile([P, H], U8, name="w1_scale", align_bytes=64)
         nc.vector.quantize_mx(out=w1_codes[:].bitcast(FP8X4), scales=w1_scale[:], in_=w1_grouped[:])
+        page.append(load_page(2, "w1_grouped"))
 
         x_codes = keep.tile([P, S], U32, name="x_codes", align_bytes=64)
         token_pieces = ((0, P), (P, S - P), (S - P, S))
         for lo, hi in token_pieces:
             nc.vector.tensor_copy(x_codes[:, lo:hi], words_all[:].bitcast(U32).indirect(offs_sb[:, lo // LANES : hi // LANES]))
+        w2_raw = keep.tile([P, PACK, N], F32, name="w2_raw", tag="words_all", align_bytes=64)
+        nc.sync.dma_start(w2_raw[:], w2.rearrange("(p j) c -> p j c", j=PACK))
 
         for t in range(PACK):
             y = keep.tile([P, S], F32, name="y%d" % t, align_bytes=64)
@@ -92,43 +106,34 @@ def tile_picked_pageread_none_p_kernel(tc, x_words, x_scales, w1, mem, w2, offs,
                 nc.scalar.copy(y[:, tokens], bank[:, :width])
             for lo, hi in ((0, P), (P, S)) if t == 0 else ((0, S),):
                 nc.vector.tensor_copy(page[t][:].indirect(slot_sb[:, lo // LANES : hi // LANES]), y[:, lo:hi])
+            if t == 0:
+                page.append(load_page(3, "y0"))
 
+        w2_grouped = keep.tile([P, N * PACK], BF16, name="w2_grouped", align_bytes=64)
+        nc.gpsimd.tensor_scalar(w2_grouped[:].rearrange("p (c j) -> p c j", j=PACK), w2_raw[:].rearrange("p j c -> p c j"), 1.0, 0.0, MULT, ADD)
+        grouped = keep.tile([P, PACK * V], BF16, name="grouped", tag="words_all", align_bytes=64)
         strips = keep.tile([P, (PACK - 1) * V], BF16, name="strips", align_bytes=64)
-        grouped = [keep.tile([P, PACK * CHUNK], BF16, name="grouped%d" % c, align_bytes=64) for c in range(CHUNKS)]
         z_codes = keep.tile([P, V], U32, name="z_codes", align_bytes=64)
         z_scale = keep.tile([P, V], U8, name="z_scale", align_bytes=64)
         out_rows = out.rearrange("(g p) v -> p g v", p=P)
 
-        def gather_views(t, lo, width):
+        def gather(t, lo, width):
             first = STRIP_OF_PLANE[t] * V + lo
             reads = rd_sb[:, lo // LANES : (lo + width) // LANES]
-            return strips[:, first : first + width], page[t][:].indirect(reads)
-
-        def gather(t, lo, width):
-            nc.scalar.activation(*gather_views(t, lo, width), COPY)
+            nc.scalar.activation(strips[:, first : first + width], page[t][:].indirect(reads), COPY)
 
         def pair_views(c, t, lo=0, width=CHUNK):
             strip = STRIP_OF_PLANE[t]
             first = c * CHUNK + lo
             src = strips[:].rearrange("p (s v) -> p v s", v=V)[:, first : first + width, strip : strip + 2]
-            dst = grouped[c][:].rearrange("p (v t) -> p v t", t=PACK)[:, lo : lo + width, t : t + 2]
+            dst = grouped[:].rearrange("p (v t) -> p v t", t=PACK)[:, first : first + width, t : t + 2]
             return dst, src
 
-        w2_grouped = keep.tile([P, N * PACK], BF16, name="w2_grouped", align_bytes=64)
-        nc.gpsimd.tensor_scalar(
-            w2_grouped[:].rearrange("p (c j) -> p c j", j=PACK),
-            w2_raw[:].rearrange("p j c -> p c j"),
-            1.0,
-            0.0,
-            mybir.AluOpType.mult,
-            mybir.AluOpType.add,
-        )
         for t in (0, 1):
             for lo in (0, V // 2):
                 gather(t, lo, V // 2)
         for c in range(CHUNKS):
-            dst, src = pair_views(c, 0)
-            nc.gpsimd.tensor_scalar(dst, src, 1.0, 0.0, mybir.AluOpType.mult, mybir.AluOpType.add)
+            nc.gpsimd.tensor_scalar(*pair_views(c, 0), 1.0, 0.0, MULT, ADD)
 
         for lo in (0, V // 2):
             gather(2, lo, V // 2)
@@ -140,7 +145,7 @@ def tile_picked_pageread_none_p_kernel(tc, x_words, x_scales, w1, mem, w2, offs,
 
         def quantize(c, lo=0, width=CHUNK):
             cols = slice(c * CHUNK + lo, c * CHUNK + lo + width)
-            nc.vector.quantize_mx(out=z_codes[:, cols].bitcast(FP8X4), scales=z_scale[:, cols], in_=grouped[c][:, PACK * lo : PACK * (lo + width)])
+            nc.vector.quantize_mx(out=z_codes[:, cols].bitcast(FP8X4), scales=z_scale[:, cols], in_=grouped[:, PACK * cols.start : PACK * cols.stop])
 
         def multiply(dst, group, first_col, width):
             rows = slice(group * P, (group + 1) * P)
@@ -165,29 +170,24 @@ def tile_picked_pageread_none_p_kernel(tc, x_words, x_scales, w1, mem, w2, offs,
             nc.vector.quantize_mx(out=w2_codes[:, rows].bitcast(FP8X4), scales=w2_scale[:, rows], in_=w2_grouped[:, PACK * rows.start : PACK * rows.stop])
 
         piece = CHUNK // 2
-        nc.vector.tensor_copy(*gather_views(3, 0, CHUNK))
-        for c in range(1, CHUNKS):
+        for c in range(CHUNKS):
             gather(3, c * CHUNK, CHUNK)
-        nc.scalar.copy(*pair_views(2, 2, 192, 64))
-        quantize_w2(0, 2)
+        quantize_w2(0, PACK)
         weave(0, 0, piece)
         weave(0, piece, piece)
         quantize(0, 0, piece)
-        quantize(0, piece, piece)
-        quantize_w2(2, 1)
         weave(1, 0, piece)
+        quantize(0, piece, piece)
         weave(1, piece, piece)
-        quantize_w2(3, 1)
-        quantize(1, 0, piece)
-        quantize(1, piece, piece)
-        weave(2, 0, 192)
+        weave(2)
+        quantize(1)
         weave(3)
         quantize(2)
         quantize(3)
         for c in (0, 1):
             for g in range(PACK):
                 bank = psum.tile([P, BANK], F32, name="bank")
-                for lo, width in ((0, piece), (piece, piece)) if g == 0 else ((0, CHUNK),):
+                for lo, width in ((0, piece), (piece, piece)) if (c, g) == (0, 0) else ((0, CHUNK),):
                     multiply(bank[:, lo : lo + width], g, c * CHUNK + lo, width)
                 store(bank, g, c * CHUNK, CHUNK, nc.scalar.copy)
         first_wide = keep.tile([P, 2 * CHUNK], F32, name="first_wide", align_bytes=64)

@@ -77,14 +77,14 @@ def tile_picked_pageread_none_p_kernel(tc, x_words, x_scales, w1, mem, w2, offs,
         w1_codes = keep.tile([P, H], U32, name="w1_codes", align_bytes=64)
         w1_scale = keep.tile([P, H], U8, name="w1_scale", align_bytes=64)
         nc.vector.quantize_mx(out=w1_codes[:].bitcast(FP8X4), scales=w1_scale[:], in_=w1_grouped[:])
-        page.append(load_page(2, "w1_grouped"))
+        w2_raw = keep.tile([P, PACK, N], F32, name="w2_raw", tag="w1_grouped", align_bytes=64)
+        nc.sync.dma_start(w2_raw[:], w2.rearrange("(p j) c -> p j c", j=PACK))
 
         x_codes = keep.tile([P, S], U32, name="x_codes", align_bytes=64)
         token_pieces = ((0, P), (P, S - P), (S - P, S))
         for lo, hi in token_pieces:
             nc.vector.tensor_copy(x_codes[:, lo:hi], words_all[:].bitcast(U32).indirect(offs_sb[:, lo // LANES : hi // LANES]))
-        w2_raw = keep.tile([P, PACK, N], F32, name="w2_raw", tag="words_all", align_bytes=64)
-        nc.sync.dma_start(w2_raw[:], w2.rearrange("(p j) c -> p j c", j=PACK))
+        page.append(load_page(2, "words_all"))
 
         for t in range(PACK):
             y = keep.tile([P, S], F32, name="y%d" % t, align_bytes=64)
@@ -111,7 +111,7 @@ def tile_picked_pageread_none_p_kernel(tc, x_words, x_scales, w1, mem, w2, offs,
 
         w2_grouped = keep.tile([P, N * PACK], BF16, name="w2_grouped", align_bytes=64)
         nc.gpsimd.tensor_scalar(w2_grouped[:].rearrange("p (c j) -> p c j", j=PACK), w2_raw[:].rearrange("p j c -> p c j"), 1.0, 0.0, MULT, ADD)
-        grouped = keep.tile([P, PACK * V], BF16, name="grouped", tag="words_all", align_bytes=64)
+        grouped = keep.tile([P, PACK * V], BF16, name="grouped", tag="w1_grouped", align_bytes=64)
         strips = keep.tile([P, (PACK - 1) * V], BF16, name="strips", align_bytes=64)
         z_codes = keep.tile([P, V], U32, name="z_codes", align_bytes=64)
         z_scale = keep.tile([P, V], U8, name="z_scale", align_bytes=64)
@@ -132,8 +132,8 @@ def tile_picked_pageread_none_p_kernel(tc, x_words, x_scales, w1, mem, w2, offs,
         for t in (0, 1):
             for lo in (0, V // 2):
                 gather(t, lo, V // 2)
-        for c in range(CHUNKS):
-            nc.gpsimd.tensor_scalar(*pair_views(c, 0), 1.0, 0.0, MULT, ADD)
+        for c, width in ((0, CHUNK), (1, V - CHUNK)):
+            nc.gpsimd.tensor_scalar(*pair_views(c, 0, 0, width), 1.0, 0.0, MULT, ADD)
 
         for lo in (0, V // 2):
             gather(2, lo, V // 2)
@@ -176,9 +176,8 @@ def tile_picked_pageread_none_p_kernel(tc, x_words, x_scales, w1, mem, w2, offs,
         weave(0, 0, piece)
         weave(0, piece, piece)
         quantize(0, 0, piece)
-        weave(1, 0, piece)
         quantize(0, piece, piece)
-        weave(1, piece, piece)
+        weave(1)
         weave(2)
         quantize(1)
         weave(3)

@@ -141,7 +141,8 @@ def tile_picked_pageread_none_p_kernel(tc, x_words, x_scales, w1, mem, w2, offs,
         w2_scale = keep.tile([P, N], U8, name="w2_scale", align_bytes=64)
 
         def weave(c, lo=0, width=CHUNK):
-            nc.vector.tensor_copy(*pair_views(c, 2, lo, width))
+            dst, src = pair_views(c, 2, lo, width)
+            nc.vector.tensor_copy(dst.rearrange("p (c i) t -> p c t i", i=4), src.rearrange("p (c i) t -> p c t i", i=4))
 
         def quantize(c, lo=0, width=CHUNK):
             cols = slice(c * CHUNK + lo, c * CHUNK + lo + width)

@@ -62,7 +62,9 @@ def tile_picked_pageread_none_p_kernel(tc, x_words, x_scales, w1, mem, w2, offs,
 
         def load_page(t, after):
             plane = keep.tile([P, U], F32, name="page%d" % t, tag=after, align_bytes=64)
-            nc.sync.dma_start(plane[:], mem_planes[t])
+            step = U // (1, 1, 2, 1)[t]
+            for lo in range(0, U, step):
+                nc.sync.dma_start(plane[:, lo : lo + step], mem_planes[t][:, lo : lo + step])
             return plane
 
         page = [load_page(0, "scales_all")]
@@ -78,7 +80,8 @@ def tile_picked_pageread_none_p_kernel(tc, x_words, x_scales, w1, mem, w2, offs,
         w1_scale = keep.tile([P, H], U8, name="w1_scale", align_bytes=64)
         nc.vector.quantize_mx(out=w1_codes[:].bitcast(FP8X4), scales=w1_scale[:], in_=w1_grouped[:])
         w2_raw = keep.tile([P, PACK, N], F32, name="w2_raw", tag="w1_grouped", align_bytes=64)
-        nc.sync.dma_start(w2_raw[:], w2.rearrange("(p j) c -> p j c", j=PACK))
+        for j in range(0, PACK, 1):
+            nc.sync.dma_start(w2_raw[:, j : j + 1], w2.rearrange("(p j) c -> p j c", j=PACK)[:, j : j + 1])
 
         x_codes = keep.tile([P, S], U32, name="x_codes", align_bytes=64)
         token_pieces = ((0, P), (P, S - P), (S - P, S))

@@ -62,7 +62,7 @@ def tile_picked_pageread_none_p_kernel(tc, x_words, x_scales, w1, mem, w2, offs,
 
         def load_page(t, after):
             plane = keep.tile([P, U], F32, name="page%d" % t, tag=after, align_bytes=64)
-            step = U // (1, 1, 2, 1)[t]
+            step = U
             for lo in range(0, U, step):
                 nc.sync.dma_start(plane[:, lo : lo + step], mem_planes[t][:, lo : lo + step])
             return plane
@@ -80,8 +80,9 @@ def tile_picked_pageread_none_p_kernel(tc, x_words, x_scales, w1, mem, w2, offs,
         w1_scale = keep.tile([P, H], U8, name="w1_scale", align_bytes=64)
         nc.vector.quantize_mx(out=w1_codes[:].bitcast(FP8X4), scales=w1_scale[:], in_=w1_grouped[:])
         w2_raw = keep.tile([P, PACK, N], F32, name="w2_raw", tag="w1_grouped", align_bytes=64)
-        for j in range(0, PACK, 1):
-            nc.sync.dma_start(w2_raw[:, j : j + 1], w2.rearrange("(p j) c -> p j c", j=PACK)[:, j : j + 1])
+        for j in range(PACK):
+            for lo in (0, N // 2):
+                nc.sync.dma_start(w2_raw[:, j, lo : lo + N // 2], w2.rearrange("(p j) c -> p j c", j=PACK)[:, j, lo : lo + N // 2])
 
         x_codes = keep.tile([P, S], U32, name="x_codes", align_bytes=64)
         token_pieces = ((0, P), (P, S - P), (S - P, S))
@@ -164,11 +165,6 @@ def tile_picked_pageread_none_p_kernel(tc, x_words, x_scales, w1, mem, w2, offs,
                 stop=True,
             )
 
-        def store(bank, group, first_col, width, copy):
-            result = keep.tile([P, width], F32, name="result%d_%d" % (first_col, group), align_bytes=64)
-            copy(result[:], bank[:, :width])
-            nc.sync.dma_start(out_rows[:, group, first_col : first_col + width], result[:])
-
         def quantize_w2(first_group, groups):
             rows = slice(first_group * P, (first_group + groups) * P)
             nc.vector.quantize_mx(out=w2_codes[:, rows].bitcast(FP8X4), scales=w2_scale[:, rows], in_=w2_grouped[:, PACK * rows.start : PACK * rows.stop])
@@ -187,19 +183,37 @@ def tile_picked_pageread_none_p_kernel(tc, x_words, x_scales, w1, mem, w2, offs,
         weave(3)
         quantize(2)
         quantize(3)
-        for c in (0, 1):
-            for g in range(PACK):
-                bank = psum.tile([P, BANK], F32, name="bank")
-                for lo, width in ((0, piece), (piece, piece)) if (c, g) == (0, 0) else ((0, CHUNK),):
-                    multiply(bank[:, lo : lo + width], g, c * CHUNK + lo, width)
-                store(bank, g, c * CHUNK, CHUNK, nc.scalar.copy)
-        first_wide = keep.tile([P, 2 * CHUNK], F32, name="first_wide", align_bytes=64)
-        for c in (2, 3):
+        results = [keep.tile([P, V], F32, name="result%d" % g, align_bytes=64) for g in range(PACK)]
+
+        def empty(copy, g, first, chunks=1):
+            lo, width = first * CHUNK, chunks * CHUNK
             bank = psum.tile([P, BANK], F32, name="bank")
-            multiply(bank[:, :CHUNK], 0, c * CHUNK, CHUNK)
-            nc.vector.tensor_copy(first_wide[:, (c - 2) * CHUNK : (c - 1) * CHUNK], bank[:, :CHUNK])
-        nc.sync.dma_start(out_rows[:, 0, 2 * CHUNK :], first_wide[:])
-        for g in range(1, PACK):
-            bank = psum.tile([P, BANK], F32, name="bank")
-            multiply(bank[:], g, 2 * CHUNK, 2 * CHUNK)
-            store(bank, g, 2 * CHUNK, 2 * CHUNK, nc.vector.tensor_copy if g % 2 == 0 else nc.scalar.copy)
+            step = piece if (g, first) == (0, 0) else width
+            for at in range(0, width, step):
+                multiply(bank[:, at : at + step], g, lo + at, step)
+            copy(results[g][:, lo : lo + width], bank[:, :width])
+
+        def store(g, first, last):
+            cols = slice(first * CHUNK, (last + 1) * CHUNK)
+            nc.sync.dma_start(out_rows[:, g, cols], results[g][:, cols])
+
+        scalar, vector = nc.scalar.copy, nc.vector.tensor_copy
+        for g in range(3):
+            empty(scalar, g, 0)
+            store(g, 0, 0)
+        empty(scalar, 3, 0)
+        empty(scalar, 3, 1)
+        store(3, 0, 1)
+        empty(scalar, 0, 1)
+        empty(scalar, 0, 2)
+        store(0, 1, 2)
+        empty(vector, 1, 1, 2)
+        empty(scalar, 2, 1, 2)
+        empty(vector, 1, 3)
+        store(1, 1, 3)
+        empty(scalar, 2, 3)
+        store(2, 1, 3)
+        empty(vector, 3, 2, 2)
+        store(3, 2, 3)
+        empty(scalar, 0, 3)
+        store(0, 3, 3)

@@ -62,7 +62,7 @@ def tile_picked_pageread_none_p_kernel(tc, x_words, x_scales, w1, mem, w2, offs,
 
         def load_page(t, after):
             plane = keep.tile([P, U], F32, name="page%d" % t, tag=after, align_bytes=64)
-            step = U
+            step = U // (1, 1, 2, 1)[t]
             for lo in range(0, U, step):
                 nc.sync.dma_start(plane[:, lo : lo + step], mem_planes[t][:, lo : lo + step])
             return plane
@@ -80,9 +80,8 @@ def tile_picked_pageread_none_p_kernel(tc, x_words, x_scales, w1, mem, w2, offs,
         w1_scale = keep.tile([P, H], U8, name="w1_scale", align_bytes=64)
         nc.vector.quantize_mx(out=w1_codes[:].bitcast(FP8X4), scales=w1_scale[:], in_=w1_grouped[:])
         w2_raw = keep.tile([P, PACK, N], F32, name="w2_raw", tag="w1_grouped", align_bytes=64)
-        for j in range(PACK):
-            for lo in (0, N // 2):
-                nc.sync.dma_start(w2_raw[:, j, lo : lo + N // 2], w2.rearrange("(p j) c -> p j c", j=PACK)[:, j, lo : lo + N // 2])
+        for j in range(0, PACK, 1):
+            nc.sync.dma_start(w2_raw[:, j : j + 1], w2.rearrange("(p j) c -> p j c", j=PACK)[:, j : j + 1])
 
         x_codes = keep.tile([P, S], U32, name="x_codes", align_bytes=64)
         token_pieces = ((0, P), (P, S - P), (S - P, S))
@@ -170,50 +169,76 @@ def tile_picked_pageread_none_p_kernel(tc, x_words, x_scales, w1, mem, w2, offs,
             nc.vector.quantize_mx(out=w2_codes[:, rows].bitcast(FP8X4), scales=w2_scale[:, rows], in_=w2_grouped[:, PACK * rows.start : PACK * rows.stop])
 
         piece = CHUNK // 2
-        for c in range(CHUNKS):
-            gather(3, c * CHUNK, CHUNK)
-        quantize_w2(0, PACK)
-        weave(0, 0, piece)
-        weave(0, piece, piece)
-        quantize(0, 0, piece)
-        quantize(0, piece, piece)
-        weave(1)
-        weave(2)
-        quantize(1)
-        weave(3)
-        quantize(2)
-        quantize(3)
         results = [keep.tile([P, V], F32, name="result%d" % g, align_bytes=64) for g in range(PACK)]
 
-        def empty(copy, g, first, chunks=1):
-            lo, width = first * CHUNK, chunks * CHUNK
-            bank = psum.tile([P, BANK], F32, name="bank")
-            step = piece if (g, first) == (0, 0) else width
-            for at in range(0, width, step):
-                multiply(bank[:, at : at + step], g, lo + at, step)
-            copy(results[g][:, lo : lo + width], bank[:, :width])
+        def weave_piece(i):
+            weave(0, i * piece, piece)
 
-        def store(g, first, last):
-            cols = slice(first * CHUNK, (last + 1) * CHUNK)
+        def quantize_piece(i):
+            quantize(0, i * piece, piece)
+
+        def product(g, first, end, widths=None):
+            lo, width = first * piece, (end - first) * piece
+            bank = psum.tile([P, BANK], F32, name="bank")
+            at = 0
+            for pieces in widths or (end - first,):
+                multiply(bank[:, at : at + pieces * piece], g, lo + at, pieces * piece)
+                at = at + pieces * piece
+            return results[g][:, lo : lo + width], bank[:, :width]
+
+        def store(g, first, end):
+            cols = slice(first * piece, end * piece)
             nc.sync.dma_start(out_rows[:, g, cols], results[g][:, cols])
 
         scalar, vector = nc.scalar.copy, nc.vector.tensor_copy
-        for g in range(3):
-            empty(scalar, g, 0)
-            store(g, 0, 0)
-        empty(scalar, 3, 0)
-        empty(scalar, 3, 1)
-        store(3, 0, 1)
-        empty(scalar, 0, 1)
-        empty(scalar, 0, 2)
-        store(0, 1, 2)
-        empty(vector, 1, 1, 2)
-        empty(scalar, 2, 1, 2)
-        empty(vector, 1, 3)
-        store(1, 1, 3)
-        empty(scalar, 2, 3)
-        store(2, 1, 3)
-        empty(vector, 3, 2, 2)
-        store(3, 2, 3)
-        empty(scalar, 0, 3)
-        store(0, 3, 3)
+        gather(3, 0 * CHUNK, CHUNK)
+        gather(3, 1 * CHUNK, CHUNK)
+        gather(3, 2 * CHUNK, CHUNK)
+        gather(3, 3 * CHUNK, CHUNK)
+        quantize_w2(0, 4)
+        weave_piece(0)
+        weave_piece(1)
+        quantize_piece(0)
+        quantize_piece(1)
+        scalar(*product(0, 0, 1))
+        store(0, 0, 1)
+        scalar(*product(1, 0, 1))
+        store(1, 0, 1)
+        scalar(*product(2, 0, 2, (1, 1,)))
+        store(2, 0, 2)
+        scalar(*product(3, 0, 2))
+        store(3, 0, 2)
+        scalar(*product(0, 1, 2))
+        weave_piece(2)
+        weave_piece(3)
+        quantize_piece(2)
+        weave_piece(4)
+        quantize_piece(3)
+        scalar(*product(0, 2, 3))
+        store(0, 1, 3)
+        scalar(*product(1, 1, 4, (1, 1, 1,)))
+        store(1, 1, 4)
+        scalar(*product(2, 2, 4))
+        weave_piece(5)
+        quantize_piece(4)
+        weave_piece(6)
+        quantize_piece(5)
+        scalar(*product(2, 4, 5))
+        store(2, 2, 5)
+        held0 = product(3, 2, 4)
+        scalar(*product(3, 4, 6, (1, 1,)))
+        weave_piece(7)
+        quantize_piece(6)
+        quantize_piece(7)
+        vector(*held0)
+        store(3, 2, 6)
+        held1 = product(0, 3, 6, (1, 2))
+        scalar(*product(0, 6, 8, (1, 1,)))
+        vector(*held1)
+        store(0, 3, 8)
+        vector(*product(1, 4, 8))
+        store(1, 4, 8)
+        scalar(*product(2, 5, 8, (1, 1, 1,)))
+        store(2, 5, 8)
+        vector(*product(3, 6, 8))
+        store(3, 6, 8)

@@ -19,12 +19,11 @@ ADD = mybir.AluOpType.add
 P = 128
 PACK = 4
 LANES = 16
-CHUNK = 256
-CHUNKS = V // CHUNK
 BANK = 512
 QUADRANT = 32
+PIECE = 128
+PIECES = V // PIECE
 W1_VECTOR_M = 48
-STRIP_OF_PLANE = (1, 2, 0, 1)
 
 
 def tile_picked_pageread_none_p_kernel(tc, x_words, x_scales, w1, mem, w2, offs, slot, rd, out):
@@ -32,6 +31,7 @@ def tile_picked_pageread_none_p_kernel(tc, x_words, x_scales, w1, mem, w2, offs,
     with ExitStack() as ctx:
         lists = ctx.enter_context(tc.tile_pool(name="lists", bufs=1))
         keep = ctx.enter_context(tc.tile_pool(name="keep", bufs=1))
+        shared = ctx.enter_context(tc.tile_pool(name="shared", bufs=1))
         psum = ctx.enter_context(tc.psum_pool(name="psum", bufs=8))
 
         offs_sb = lists.tile([P, S // LANES], U16, name="offs_sb")
@@ -42,7 +42,23 @@ def tile_picked_pageread_none_p_kernel(tc, x_words, x_scales, w1, mem, w2, offs,
         w1_raw = keep.tile([P, PACK, H], F32, name="w1_raw", align_bytes=64)
         x_scale = keep.tile([P, S], U8, name="x_scale", align_bytes=64)
         w1_rows = w1.rearrange("(p j) c -> p j c", j=PACK)
+        w2_rows = w2.rearrange("(p j) c -> p j c", j=PACK)
         mem_planes = mem.rearrange("(p t) u -> t p u", t=PACK)
+        out_rows = out.rearrange("(g p) v -> p g v", p=P)
+
+        def entries(tile, lo, hi):
+            return tile[:, lo // LANES : hi // LANES]
+
+        def multiply(dst, codes, scale, rows, rhs, rhs_scale, cols):
+            nc.tensor.matmul_mx(
+                out=dst,
+                lhsT=codes[:, rows].bitcast(FP8X4),
+                lhsT_scale=scale[:, rows],
+                rhs=rhs[:, cols].bitcast(FP8X4),
+                rhs_scale=rhs_scale[:, cols],
+                start=True,
+                stop=True,
+            )
 
         nc.vector.memset(scales_all[:].bitcast(I32), 0)
         nc.vector.memset(x_scale[:].bitcast(I32), 0)
@@ -60,16 +76,19 @@ def tile_picked_pageread_none_p_kernel(tc, x_words, x_scales, w1, mem, w2, offs,
             first = 32 + 16 * q
             nc.sync.dma_start(x_scale[QUADRANT * q : QUADRANT * q + 4, :].bitcast(I32), picked_scales[first : first + 16 : 4, :].bitcast(I32))
 
-        def load_page(t, after):
-            plane = keep.tile([P, U], F32, name="page%d" % t, tag=after, align_bytes=64)
-            step = U // (1, 1, 2, 1)[t]
+        def load_page(t, after, loads=1):
+            if after is None:
+                plane = shared.tile([P, U], F32, name="page%d" % t, offset=0, align_bytes=64)
+            else:
+                plane = keep.tile([P, U], F32, name="page%d" % t, tag=after, align_bytes=64)
+            step = U // loads
             for lo in range(0, U, step):
                 nc.sync.dma_start(plane[:, lo : lo + step], mem_planes[t][:, lo : lo + step])
             return plane
 
         page = [load_page(0, "scales_all")]
 
-        w1_grouped = keep.tile([P, H * PACK], BF16, name="w1_grouped", align_bytes=64)
+        w1_grouped = shared.tile([P, H * PACK], BF16, name="w1_grouped", offset=0, align_bytes=64)
         w1_dst = w1_grouped[:].rearrange("p (t m j) -> p m t j", t=PACK, j=PACK)
         w1_src = w1_raw[:].rearrange("p j (m t) -> p m t j", t=PACK)
         nc.vector.tensor_copy(w1_dst[:, :W1_VECTOR_M], w1_src[:, :W1_VECTOR_M])
@@ -79,166 +98,127 @@ def tile_picked_pageread_none_p_kernel(tc, x_words, x_scales, w1, mem, w2, offs,
         w1_codes = keep.tile([P, H], U32, name="w1_codes", align_bytes=64)
         w1_scale = keep.tile([P, H], U8, name="w1_scale", align_bytes=64)
         nc.vector.quantize_mx(out=w1_codes[:].bitcast(FP8X4), scales=w1_scale[:], in_=w1_grouped[:])
-        w2_raw = keep.tile([P, PACK, N], F32, name="w2_raw", tag="w1_grouped", align_bytes=64)
-        for j in range(0, PACK, 1):
-            nc.sync.dma_start(w2_raw[:, j : j + 1], w2.rearrange("(p j) c -> p j c", j=PACK)[:, j : j + 1])
+        w2_raw = shared.tile([P, PACK, N], F32, name="w2_raw", offset=0, align_bytes=64)
+        for j in range(PACK):
+            nc.sync.dma_start(w2_raw[:, j : j + 1], w2_rows[:, j : j + 1])
 
         x_codes = keep.tile([P, S], U32, name="x_codes", align_bytes=64)
         token_pieces = ((0, P), (P, S - P), (S - P, S))
         for lo, hi in token_pieces:
-            nc.vector.tensor_copy(x_codes[:, lo:hi], words_all[:].bitcast(U32).indirect(offs_sb[:, lo // LANES : hi // LANES]))
-        page.append(load_page(2, "words_all"))
-
-        for t in range(PACK):
-            y = keep.tile([P, S], F32, name="y%d" % t, align_bytes=64)
-            features = slice(t * P, (t + 1) * P)
-            products = token_pieces if t == 0 else ((0, S),)
-            for lo, hi in products:
-                tokens = slice(lo, hi)
-                width = hi - lo
-                bank = psum.tile([P, BANK], F32, name="bank")
-                nc.tensor.matmul_mx(
-                    out=bank[:, :width],
-                    lhsT=w1_codes[:, features].bitcast(FP8X4),
-                    lhsT_scale=w1_scale[:, features],
-                    rhs=x_codes[:, tokens].bitcast(FP8X4),
-                    rhs_scale=x_scale[:, tokens],
-                    start=True,
-                    stop=True,
-                )
-                nc.scalar.copy(y[:, tokens], bank[:, :width])
-            for lo, hi in ((0, P), (P, S)) if t == 0 else ((0, S),):
-                nc.vector.tensor_copy(page[t][:].indirect(slot_sb[:, lo // LANES : hi // LANES]), y[:, lo:hi])
-            if t == 0:
-                page.append(load_page(3, "y0"))
+            nc.vector.tensor_copy(x_codes[:, lo:hi], words_all[:].bitcast(U32).indirect(entries(offs_sb, lo, hi)))
+        page.append(load_page(2, "words_all", loads=2))
 
         w2_grouped = keep.tile([P, N * PACK], BF16, name="w2_grouped", align_bytes=64)
         nc.gpsimd.tensor_scalar(w2_grouped[:].rearrange("p (c j) -> p c j", j=PACK), w2_raw[:].rearrange("p j c -> p c j"), 1.0, 0.0, MULT, ADD)
-        grouped = keep.tile([P, PACK * V], BF16, name="grouped", tag="w1_grouped", align_bytes=64)
-        strips = keep.tile([P, (PACK - 1) * V], BF16, name="strips", align_bytes=64)
+        page.append(load_page(3, None))
+
+        for t in range(PACK):
+            y = keep.tile([P, S], F32, name="y%d" % t, align_bytes=64)
+            for lo, hi in token_pieces if t == 0 else ((0, S),):
+                bank = psum.tile([P, BANK], F32, name="bank")
+                multiply(bank[:, : hi - lo], w1_codes, w1_scale, slice(t * P, (t + 1) * P), x_codes, x_scale, slice(lo, hi))
+                nc.scalar.copy(y[:, lo:hi], bank[:, : hi - lo])
+            for lo, hi in ((0, P), (P, S)) if t == 0 else ((0, S),):
+                nc.vector.tensor_copy(page[t][:].indirect(entries(slot_sb, lo, hi)), y[:, lo:hi])
+
+        grouped = shared.tile([P, PACK * V], BF16, name="grouped", offset=4 * U, align_bytes=64)
+        strips = keep.tile([P, 2 * V], F32, name="strips", align_bytes=64)
+        early = strips[:, V:].bitcast(BF16)
         z_codes = keep.tile([P, V], U32, name="z_codes", align_bytes=64)
         z_scale = keep.tile([P, V], U8, name="z_scale", align_bytes=64)
-        out_rows = out.rearrange("(g p) v -> p g v", p=P)
+        woven = grouped[:].rearrange("p (v t) -> p v t", t=PACK)
 
-        def gather(t, lo, width):
-            first = STRIP_OF_PLANE[t] * V + lo
-            reads = rd_sb[:, lo // LANES : (lo + width) // LANES]
-            nc.scalar.activation(strips[:, first : first + width], page[t][:].indirect(reads), COPY)
-
-        def pair_views(c, t, lo=0, width=CHUNK):
-            strip = STRIP_OF_PLANE[t]
-            first = c * CHUNK + lo
-            src = strips[:].rearrange("p (s v) -> p v s", v=V)[:, first : first + width, strip : strip + 2]
-            dst = grouped[:].rearrange("p (v t) -> p v t", t=PACK)[:, first : first + width, t : t + 2]
-            return dst, src
+        def gather(t, lo, hi):
+            dst = early if t < 2 else strips[:]
+            first = t % 2 * V
+            nc.scalar.activation(dst[:, first + lo : first + hi], page[t][:].indirect(entries(rd_sb, lo, hi)), COPY)
 
         for t in (0, 1):
             for lo in (0, V // 2):
-                gather(t, lo, V // 2)
-        for c, width in ((0, CHUNK), (1, V - CHUNK)):
-            nc.gpsimd.tensor_scalar(*pair_views(c, 0, 0, width), 1.0, 0.0, MULT, ADD)
-
+                gather(t, lo, lo + V // 2)
+        for lo, hi in ((0, 2 * PIECE), (2 * PIECE, V)):
+            nc.gpsimd.tensor_scalar(woven[:, lo:hi, :2], early.rearrange("p (s v) -> p v s", v=V)[:, lo:hi], 1.0, 0.0, MULT, ADD)
         for lo in (0, V // 2):
-            gather(2, lo, V // 2)
+            gather(2, lo, lo + V // 2)
+
         w2_codes = keep.tile([P, N], U32, name="w2_codes", tag="y3", align_bytes=64)
         w2_scale = keep.tile([P, N], U8, name="w2_scale", align_bytes=64)
-
-        def weave(c, lo=0, width=CHUNK):
-            dst, src = pair_views(c, 2, lo, width)
-            nc.vector.tensor_copy(dst.rearrange("p (c i) t -> p c t i", i=4), src.rearrange("p (c i) t -> p c t i", i=4))
-
-        def quantize(c, lo=0, width=CHUNK):
-            cols = slice(c * CHUNK + lo, c * CHUNK + lo + width)
-            nc.vector.quantize_mx(out=z_codes[:, cols].bitcast(FP8X4), scales=z_scale[:, cols], in_=grouped[:, PACK * cols.start : PACK * cols.stop])
-
-        def multiply(dst, group, first_col, width):
-            rows = slice(group * P, (group + 1) * P)
-            cols = slice(first_col, first_col + width)
-            nc.tensor.matmul_mx(
-                out=dst,
-                lhsT=w2_codes[:, rows].bitcast(FP8X4),
-                lhsT_scale=w2_scale[:, rows],
-                rhs=z_codes[:, cols].bitcast(FP8X4),
-                rhs_scale=z_scale[:, cols],
-                start=True,
-                stop=True,
-            )
-
-        def quantize_w2(first_group, groups):
-            rows = slice(first_group * P, (first_group + groups) * P)
-            nc.vector.quantize_mx(out=w2_codes[:, rows].bitcast(FP8X4), scales=w2_scale[:, rows], in_=w2_grouped[:, PACK * rows.start : PACK * rows.stop])
-
-        piece = CHUNK // 2
         results = [keep.tile([P, V], F32, name="result%d" % g, align_bytes=64) for g in range(PACK)]
 
-        def weave_piece(i):
-            weave(0, i * piece, piece)
+        def weave(i):
+            cols = slice(i * PIECE, (i + 1) * PIECE)
+            src = strips[:].rearrange("p (s v) -> p v s", v=V)[:, cols]
+            nc.vector.tensor_copy(woven[:, cols, 2:].rearrange("p (c i) t -> p c t i", i=4), src.rearrange("p (c i) t -> p c t i", i=4))
 
-        def quantize_piece(i):
-            quantize(0, i * piece, piece)
+        def quantize(i):
+            cols = slice(i * PIECE, (i + 1) * PIECE)
+            nc.vector.quantize_mx(out=z_codes[:, cols].bitcast(FP8X4), scales=z_scale[:, cols], in_=grouped[:, PACK * cols.start : PACK * cols.stop])
+
+        def quantize_w2(lo, hi):
+            nc.vector.quantize_mx(out=w2_codes[:, lo:hi].bitcast(FP8X4), scales=w2_scale[:, lo:hi], in_=w2_grouped[:, PACK * lo : PACK * hi])
 
         def product(g, first, end, widths=None):
-            lo, width = first * piece, (end - first) * piece
+            lo, width = first * PIECE, (end - first) * PIECE
             bank = psum.tile([P, BANK], F32, name="bank")
             at = 0
             for pieces in widths or (end - first,):
-                multiply(bank[:, at : at + pieces * piece], g, lo + at, pieces * piece)
-                at = at + pieces * piece
+                multiply(bank[:, at : at + pieces * PIECE], w2_codes, w2_scale, slice(g * P, (g + 1) * P), z_codes, z_scale, slice(lo + at, lo + at + pieces * PIECE))
+                at = at + pieces * PIECE
             return results[g][:, lo : lo + width], bank[:, :width]
 
         def store(g, first, end):
-            cols = slice(first * piece, end * piece)
+            cols = slice(first * PIECE, end * PIECE)
             nc.sync.dma_start(out_rows[:, g, cols], results[g][:, cols])
 
         scalar, vector = nc.scalar.copy, nc.vector.tensor_copy
-        gather(3, 0 * CHUNK, CHUNK)
-        gather(3, 1 * CHUNK, CHUNK)
-        gather(3, 2 * CHUNK, CHUNK)
-        gather(3, 3 * CHUNK, CHUNK)
-        quantize_w2(0, 4)
-        weave_piece(0)
-        weave_piece(1)
-        quantize_piece(0)
-        quantize_piece(1)
+        nc.vector.tensor_copy(strips[:].bitcast(U32)[:, V : V + PIECE], page[3][:].bitcast(U32).indirect(entries(rd_sb, 0, PIECE)))
+        for first, end in ((1, 3), (3, 5), (5, 8)):
+            gather(3, first * PIECE, end * PIECE)
+        quantize_w2(0, N // 2)
+        weave(0)
+        quantize_w2(N // 2, N)
+        quantize(0)
+        weave(1)
+        weave(2)
+        quantize(1)
         scalar(*product(0, 0, 1))
         store(0, 0, 1)
         scalar(*product(1, 0, 1))
         store(1, 0, 1)
-        scalar(*product(2, 0, 2, (1, 1,)))
+        scalar(*product(2, 0, 2, (1, 1)))
         store(2, 0, 2)
         scalar(*product(3, 0, 2))
         store(3, 0, 2)
         scalar(*product(0, 1, 2))
-        weave_piece(2)
-        weave_piece(3)
-        quantize_piece(2)
-        weave_piece(4)
-        quantize_piece(3)
+        weave(3)
+        quantize(2)
+        weave(4)
+        quantize(3)
         scalar(*product(0, 2, 3))
         store(0, 1, 3)
-        scalar(*product(1, 1, 4, (1, 1, 1,)))
+        scalar(*product(1, 1, 4, (1, 1, 1)))
         store(1, 1, 4)
         scalar(*product(2, 2, 4))
-        weave_piece(5)
-        quantize_piece(4)
-        weave_piece(6)
-        quantize_piece(5)
+        weave(5)
+        quantize(4)
+        weave(6)
+        quantize(5)
         scalar(*product(2, 4, 5))
         store(2, 2, 5)
         held0 = product(3, 2, 4)
-        scalar(*product(3, 4, 6, (1, 1,)))
-        weave_piece(7)
-        quantize_piece(6)
-        quantize_piece(7)
+        scalar(*product(3, 4, 6, (1, 1)))
+        weave(7)
+        quantize(6)
+        quantize(7)
         vector(*held0)
         store(3, 2, 6)
         held1 = product(0, 3, 6, (1, 2))
-        scalar(*product(0, 6, 8, (1, 1,)))
+        scalar(*product(0, 6, 8, (1, 1)))
         vector(*held1)
         store(0, 3, 8)
         vector(*product(1, 4, 8))
         store(1, 4, 8)
-        scalar(*product(2, 5, 8, (1, 1, 1,)))
+        scalar(*product(2, 5, 8, (1, 1, 1)))
         store(2, 5, 8)
         vector(*product(3, 6, 8))
         store(3, 6, 8)

@@ -24,6 +24,7 @@ QUADRANT = 32
 PIECE = 128
 PIECES = V // PIECE
 W1_VECTOR_M = 48
+STRIP_OF_PLANE = (0, 2, 1, 2)
 
 
 def tile_picked_pageread_none_p_kernel(tc, x_words, x_scales, w1, mem, w2, offs, slot, rd, out):
@@ -122,24 +123,25 @@ def tile_picked_pageread_none_p_kernel(tc, x_words, x_scales, w1, mem, w2, offs,
                 nc.vector.tensor_copy(page[t][:].indirect(entries(slot_sb, lo, hi)), y[:, lo:hi])
 
         grouped = shared.tile([P, PACK * V], BF16, name="grouped", offset=4 * U, align_bytes=64)
-        strips = keep.tile([P, 2 * V], F32, name="strips", align_bytes=64)
-        early = strips[:, V:].bitcast(BF16)
+        strips = keep.tile([P, 3 * V], BF16, name="strips", align_bytes=64)
+        by_strip = strips[:].rearrange("p (s v) -> p v s", v=V)
+        first_reads = strips[:, V - PIECE : V + PIECE]
         z_codes = keep.tile([P, V], U32, name="z_codes", align_bytes=64)
         z_scale = keep.tile([P, V], U8, name="z_scale", align_bytes=64)
         woven = grouped[:].rearrange("p (v t) -> p v t", t=PACK)
 
         def gather(t, lo, hi):
-            dst = early if t < 2 else strips[:]
-            first = t % 2 * V
-            nc.scalar.activation(dst[:, first + lo : first + hi], page[t][:].indirect(entries(rd_sb, lo, hi)), COPY)
+            first = STRIP_OF_PLANE[t] * V
+            nc.scalar.activation(strips[:, first + lo : first + hi], page[t][:].indirect(entries(rd_sb, lo, hi)), COPY)
 
         for t in (0, 1):
             for lo in (0, V // 2):
                 gather(t, lo, lo + V // 2)
         for lo, hi in ((0, 2 * PIECE), (2 * PIECE, V)):
-            nc.gpsimd.tensor_scalar(woven[:, lo:hi, :2], early.rearrange("p (s v) -> p v s", v=V)[:, lo:hi], 1.0, 0.0, MULT, ADD)
+            nc.gpsimd.tensor_scalar(woven[:, lo:hi, :2], by_strip[:, lo:hi, ::2], 1.0, 0.0, MULT, ADD)
         for lo in (0, V // 2):
             gather(2, lo, lo + V // 2)
+        nc.scalar.copy(woven[:, :PIECE, 2], by_strip[:, :PIECE, 1])
 
         w2_codes = keep.tile([P, N], U32, name="w2_codes", tag="y3", align_bytes=64)
         w2_scale = keep.tile([P, N], U8, name="w2_scale", align_bytes=64)
@@ -147,7 +149,7 @@ def tile_picked_pageread_none_p_kernel(tc, x_words, x_scales, w1, mem, w2, offs,
 
         def weave(i):
             cols = slice(i * PIECE, (i + 1) * PIECE)
-            src = strips[:].rearrange("p (s v) -> p v s", v=V)[:, cols]
+            src = by_strip[:, cols, 1:]
             nc.vector.tensor_copy(woven[:, cols, 2:].rearrange("p (c i) t -> p c t i", i=4), src.rearrange("p (c i) t -> p c t i", i=4))
 
         def quantize(i):
@@ -157,68 +159,44 @@ def tile_picked_pageread_none_p_kernel(tc, x_words, x_scales, w1, mem, w2, offs,
         def quantize_w2(lo, hi):
             nc.vector.quantize_mx(out=w2_codes[:, lo:hi].bitcast(FP8X4), scales=w2_scale[:, lo:hi], in_=w2_grouped[:, PACK * lo : PACK * hi])
 
-        def product(g, first, end, widths=None):
-            lo, width = first * PIECE, (end - first) * PIECE
-            bank = psum.tile([P, BANK], F32, name="bank")
-            at = 0
-            for pieces in widths or (end - first,):
-                multiply(bank[:, at : at + pieces * PIECE], w2_codes, w2_scale, slice(g * P, (g + 1) * P), z_codes, z_scale, slice(lo + at, lo + at + pieces * PIECE))
-                at = at + pieces * PIECE
-            return results[g][:, lo : lo + width], bank[:, :width]
+        def empty(copy, g, first, end):
+            cols = slice(first * PIECE, end * PIECE)
+            bank = psum.tile([P, BANK], F32, name="bank")[:, : (end - first) * PIECE]
+            for lo, hi in ((first, end),) if end - first != 3 else ((first, first + 2), (first + 2, end)):
+                part = bank[:, (lo - first) * PIECE : (hi - first) * PIECE]
+                multiply(part, w2_codes, w2_scale, slice(g * P, (g + 1) * P), z_codes, z_scale, slice(lo * PIECE, hi * PIECE))
+            copy(results[g][:, cols], bank)
 
         def store(g, first, end):
             cols = slice(first * PIECE, end * PIECE)
             nc.sync.dma_start(out_rows[:, g, cols], results[g][:, cols])
 
         scalar, vector = nc.scalar.copy, nc.vector.tensor_copy
-        nc.vector.tensor_copy(strips[:].bitcast(U32)[:, V : V + PIECE], page[3][:].bitcast(U32).indirect(entries(rd_sb, 0, PIECE)))
+        nc.vector.tensor_copy(first_reads.bitcast(U32), page[3][:].bitcast(U32).indirect(entries(rd_sb, 0, PIECE)))
         for first, end in ((1, 3), (3, 5), (5, 8)):
             gather(3, first * PIECE, end * PIECE)
         quantize_w2(0, N // 2)
-        weave(0)
+        nc.vector.tensor_copy(woven[:, :PIECE, 3], first_reads.bitcast(F32))
         quantize_w2(N // 2, N)
         quantize(0)
+        for g in range(PACK):
+            empty(scalar, g, 0, 1)
+            store(g, 0, 1)
         weave(1)
-        weave(2)
-        quantize(1)
-        scalar(*product(0, 0, 1))
-        store(0, 0, 1)
-        scalar(*product(1, 0, 1))
-        store(1, 0, 1)
-        scalar(*product(2, 0, 2, (1, 1)))
-        store(2, 0, 2)
-        scalar(*product(3, 0, 2))
-        store(3, 0, 2)
-        scalar(*product(0, 1, 2))
-        weave(3)
-        quantize(2)
-        weave(4)
-        quantize(3)
-        scalar(*product(0, 2, 3))
-        store(0, 1, 3)
-        scalar(*product(1, 1, 4, (1, 1, 1)))
-        store(1, 1, 4)
-        scalar(*product(2, 2, 4))
-        weave(5)
-        quantize(4)
-        weave(6)
-        quantize(5)
-        scalar(*product(2, 4, 5))
-        store(2, 2, 5)
-        held0 = product(3, 2, 4)
-        scalar(*product(3, 4, 6, (1, 1)))
-        weave(7)
-        quantize(6)
-        quantize(7)
-        vector(*held0)
-        store(3, 2, 6)
-        held1 = product(0, 3, 6, (1, 2))
-        scalar(*product(0, 6, 8, (1, 1)))
-        vector(*held1)
-        store(0, 3, 8)
-        vector(*product(1, 4, 8))
-        store(1, 4, 8)
-        scalar(*product(2, 5, 8, (1, 1, 1)))
-        store(2, 5, 8)
-        vector(*product(3, 6, 8))
-        store(3, 6, 8)
+        for i in range(1, PIECES):
+            if i + 1 < PIECES:
+                weave(i + 1)
+            quantize(i)
+            if 0 <= i - 2 < PACK:
+                empty(scalar, i - 2, i, i + 1)
+                store(i - 2, 1, i + 1)
+            if i - 1 < PACK:
+                empty(scalar, i - 1, 1, i + 1)
+            if i == PIECES - 2:
+                held = (0, 3, i + 1)
+        empty(scalar, 0, PIECES - 1, PIECES)
+        empty(vector, *held)
+        store(0, 3, PIECES)
+        for g in range(1, PACK):
+            empty((vector, scalar)[g % 2], g, 3 + g, PIECES)
+            store(g, 3 + g, PIECES)

@@ -100,14 +100,13 @@ def tile_picked_pageread_none_p_kernel(tc, x_words, x_scales, w1, mem, w2, offs,
         w1_scale = keep.tile([P, H], U8, name="w1_scale", align_bytes=64)
         nc.vector.quantize_mx(out=w1_codes[:].bitcast(FP8X4), scales=w1_scale[:], in_=w1_grouped[:])
         w2_raw = shared.tile([P, PACK, N], F32, name="w2_raw", offset=0, align_bytes=64)
-        for j in range(PACK):
-            nc.sync.dma_start(w2_raw[:, j : j + 1], w2_rows[:, j : j + 1])
+        nc.sync.dma_start(w2_raw[:], w2_rows)
 
         x_codes = keep.tile([P, S], U32, name="x_codes", align_bytes=64)
         token_pieces = ((0, P), (P, S - P), (S - P, S))
         for lo, hi in token_pieces:
             nc.vector.tensor_copy(x_codes[:, lo:hi], words_all[:].bitcast(U32).indirect(entries(offs_sb, lo, hi)))
-        page.append(load_page(2, "words_all", loads=2))
+        page.append(load_page(2, "words_all"))
 
         w2_grouped = keep.tile([P, N * PACK], BF16, name="w2_grouped", align_bytes=64)
         nc.gpsimd.tensor_scalar(w2_grouped[:].rearrange("p (c j) -> p c j", j=PACK), w2_raw[:].rearrange("p j c -> p c j"), 1.0, 0.0, MULT, ADD)
@@ -178,25 +177,21 @@ def tile_picked_pageread_none_p_kernel(tc, x_words, x_scales, w1, mem, w2, offs,
         quantize_w2(0, N // 2)
         nc.vector.tensor_copy(woven[:, :PIECE, 3], first_reads.bitcast(F32))
         quantize_w2(N // 2, N)
-        quantize(0)
-        for g in range(PACK):
-            empty(scalar, g, 0, 1)
-            store(g, 0, 1)
-        weave(1)
-        for i in range(1, PIECES):
-            if i + 1 < PIECES:
-                weave(i + 1)
+
+        cuts = [(0, 1, 2 + g // 2, 4 + max(0, g - 1), PIECES) for g in range(PACK)]
+        last = PIECES - 1
+        for i in range(PIECES):
+            for ahead in {0: (), 1: (1, 2), last: ()}.get(i, (i + 1,)):
+                weave(ahead)
             quantize(i)
-            if 0 <= i - 2 < PACK:
-                empty(scalar, i - 2, i, i + 1)
-                store(i - 2, 1, i + 1)
-            if i - 1 < PACK:
-                empty(scalar, i - 1, 1, i + 1)
-            if i == PIECES - 2:
-                held = (0, 3, i + 1)
-        empty(scalar, 0, PIECES - 1, PIECES)
-        empty(vector, *held)
-        store(0, 3, PIECES)
+            for g in range(PACK):
+                if i < last and i + 1 in cuts[g]:
+                    first = cuts[g][cuts[g].index(i + 1) - 1]
+                    empty(scalar, g, first, i + 1)
+                    store(g, first, i + 1)
+        empty(scalar, 0, last, PIECES)
+        empty(vector, 0, cuts[0][-2], last)
+        store(0, cuts[0][-2], PIECES)
         for g in range(1, PACK):
-            empty((vector, scalar)[g % 2], g, 3 + g, PIECES)
-            store(g, 3 + g, PIECES)
+            empty((scalar, vector)[g % 2], g, cuts[g][-2], PIECES)
+            store(g, cuts[g][-2], PIECES)

from contextlib import ExitStack

import concourse.mybir as mybir

K, T, S, V, N, U, H = 512, 2048, 512, 1024, 512, 1024, 512
FLOPS = 2 * K * H * S + 2 * H * N * V

F32 = mybir.dt.float32
BF16 = mybir.dt.bfloat16
I32 = mybir.dt.int32
U32 = mybir.dt.uint32
U16 = mybir.dt.uint16
U8 = mybir.dt.uint8
FP8X4 = mybir.dt.float8_e4m3fn_x4
COPY = mybir.ActivationFunctionType.Copy
MULT = mybir.AluOpType.mult
ADD = mybir.AluOpType.add

P = 128
PACK = 4
LANES = 16
BANK = 512
QUADRANT = 32
PIECE = 128
PIECES = V // PIECE
W1_VECTOR_M = 48
STRIP_OF_PLANE = (0, 2, 1, 2)


def tile_picked_pageread_none_p_kernel(tc, x_words, x_scales, w1, mem, w2, offs, slot, rd, out):
    nc = tc.nc
    with ExitStack() as ctx:
        lists = ctx.enter_context(tc.tile_pool(name="lists", bufs=1))
        keep = ctx.enter_context(tc.tile_pool(name="keep", bufs=1))
        shared = ctx.enter_context(tc.tile_pool(name="shared", bufs=1))
        psum = ctx.enter_context(tc.psum_pool(name="psum", bufs=8))

        offs_sb = lists.tile([P, S // LANES], U16, name="offs_sb")
        slot_sb = lists.tile([P, S // LANES], U16, name="slot_sb")
        rd_sb = lists.tile([P, V // LANES], U16, name="rd_sb")
        words_all = keep.tile([P, T], I32, name="words_all", align_bytes=64)
        scales_all = keep.tile([P, T], U8, name="scales_all", align_bytes=64)
        w1_raw = keep.tile([P, PACK, H], F32, name="w1_raw", align_bytes=64)
        x_scale = keep.tile([P, S], U8, name="x_scale", align_bytes=64)
        w1_rows = w1.rearrange("(p j) c -> p j c", j=PACK)
        w2_rows = w2.rearrange("(p j) c -> p j c", j=PACK)
        mem_planes = mem.rearrange("(p t) u -> t p u", t=PACK)
        out_rows = out.rearrange("(g p) v -> p g v", p=P)

        def entries(tile, lo, hi):
            return tile[:, lo // LANES : hi // LANES]

        def multiply(dst, codes, scale, rows, rhs, rhs_scale, cols):
            nc.tensor.matmul_mx(
                out=dst,
                lhsT=codes[:, rows].bitcast(FP8X4),
                lhsT_scale=scale[:, rows],
                rhs=rhs[:, cols].bitcast(FP8X4),
                rhs_scale=rhs_scale[:, cols],
                start=True,
                stop=True,
            )

        nc.vector.memset(scales_all[:].bitcast(I32), 0)
        nc.vector.memset(x_scale[:].bitcast(I32), 0)
        nc.sync.dma_start(w1_raw[:, :1], w1_rows[:, :1])
        nc.sync.dma_start(offs_sb[:], offs)
        nc.sync.dma_start(scales_all[32:96:4, :].bitcast(I32), x_scales[0].bitcast(I32))
        nc.sync.dma_start(w1_raw[:, 1:], w1_rows[:, 1:])
        nc.sync.dma_start(words_all[:], x_words[0].rearrange("p c r -> p (c r)").bitcast(I32))
        nc.sync.dma_start(slot_sb[:], slot)
        nc.sync.dma_start(rd_sb[:], rd)

        picked_scales = keep.tile([P, S], U8, name="picked_scales", align_bytes=64)
        nc.vector.tensor_copy(picked_scales[:], scales_all[:].indirect(offs_sb[:]))
        for q in range(4):
            first = 32 + 16 * q
            nc.sync.dma_start(x_scale[QUADRANT * q : QUADRANT * q + 4, :].bitcast(I32), picked_scales[first : first + 16 : 4, :].bitcast(I32))

        def load_page(t, after, loads=1):
            if after is None:
                plane = shared.tile([P, U], F32, name="page%d" % t, offset=0, align_bytes=64)
            else:
                plane = keep.tile([P, U], F32, name="page%d" % t, tag=after, align_bytes=64)
            step = U // loads
            for lo in range(0, U, step):
                nc.sync.dma_start(plane[:, lo : lo + step], mem_planes[t][:, lo : lo + step])
            return plane

        page = [load_page(0, "scales_all")]

        w1_grouped = shared.tile([P, H * PACK], BF16, name="w1_grouped", offset=0, align_bytes=64)
        w1_dst = w1_grouped[:].rearrange("p (t m j) -> p m t j", t=PACK, j=PACK)
        w1_src = w1_raw[:].rearrange("p j (m t) -> p m t j", t=PACK)
        nc.vector.tensor_copy(w1_dst[:, :W1_VECTOR_M], w1_src[:, :W1_VECTOR_M])
        for rows in (slice(0, 1), slice(1, PACK)):
            nc.scalar.copy(w1_dst[:, W1_VECTOR_M:, :, rows], w1_src[:, W1_VECTOR_M:, :, rows])
        page.append(load_page(1, "w1_raw"))
        w1_codes = keep.tile([P, H], U32, name="w1_codes", align_bytes=64)
        w1_scale = keep.tile([P, H], U8, name="w1_scale", align_bytes=64)
        nc.vector.quantize_mx(out=w1_codes[:].bitcast(FP8X4), scales=w1_scale[:], in_=w1_grouped[:])
        w2_raw = shared.tile([P, PACK, N], F32, name="w2_raw", offset=0, align_bytes=64)
        nc.sync.dma_start(w2_raw[:], w2_rows)

        x_codes = keep.tile([P, S], U32, name="x_codes", align_bytes=64)
        token_pieces = ((0, P), (P, S - P), (S - P, S))
        for lo, hi in token_pieces:
            nc.vector.tensor_copy(x_codes[:, lo:hi], words_all[:].bitcast(U32).indirect(entries(offs_sb, lo, hi)))
        page.append(load_page(2, "words_all"))

        w2_grouped = keep.tile([P, N * PACK], BF16, name="w2_grouped", align_bytes=64)
        nc.gpsimd.tensor_scalar(w2_grouped[:].rearrange("p (c j) -> p c j", j=PACK), w2_raw[:].rearrange("p j c -> p c j"), 1.0, 0.0, MULT, ADD)
        page.append(load_page(3, None))

        for t in range(PACK):
            y = keep.tile([P, S], F32, name="y%d" % t, align_bytes=64)
            for lo, hi in token_pieces if t == 0 else ((0, S),):
                bank = psum.tile([P, BANK], F32, name="bank")
                multiply(bank[:, : hi - lo], w1_codes, w1_scale, slice(t * P, (t + 1) * P), x_codes, x_scale, slice(lo, hi))
                nc.scalar.copy(y[:, lo:hi], bank[:, : hi - lo])
            for lo, hi in ((0, P), (P, S)) if t == 0 else ((0, S),):
                nc.vector.tensor_copy(page[t][:].indirect(entries(slot_sb, lo, hi)), y[:, lo:hi])

        grouped = shared.tile([P, PACK * V], BF16, name="grouped", offset=4 * U, align_bytes=64)
        strips = keep.tile([P, 3 * V], BF16, name="strips", align_bytes=64)
        by_strip = strips[:].rearrange("p (s v) -> p v s", v=V)
        first_reads = strips[:, V - PIECE : V + PIECE]
        z_codes = keep.tile([P, V], U32, name="z_codes", align_bytes=64)
        z_scale = keep.tile([P, V], U8, name="z_scale", align_bytes=64)
        woven = grouped[:].rearrange("p (v t) -> p v t", t=PACK)

        def gather(t, lo, hi):
            first = STRIP_OF_PLANE[t] * V
            nc.scalar.activation(strips[:, first + lo : first + hi], page[t][:].indirect(entries(rd_sb, lo, hi)), COPY)

        for t in (0, 1):
            for lo in (0, V // 2):
                gather(t, lo, lo + V // 2)
        for lo, hi in ((0, 2 * PIECE), (2 * PIECE, V)):
            nc.gpsimd.tensor_scalar(woven[:, lo:hi, :2], by_strip[:, lo:hi, ::2], 1.0, 0.0, MULT, ADD)
        for lo in (0, V // 2):
            gather(2, lo, lo + V // 2)
        nc.scalar.copy(woven[:, :PIECE, 2], by_strip[:, :PIECE, 1])

        w2_codes = keep.tile([P, N], U32, name="w2_codes", tag="y3", align_bytes=64)
        w2_scale = keep.tile([P, N], U8, name="w2_scale", align_bytes=64)
        results = [keep.tile([P, V], F32, name="result%d" % g, align_bytes=64) for g in range(PACK)]

        def weave(i):
            cols = slice(i * PIECE, (i + 1) * PIECE)
            src = by_strip[:, cols, 1:]
            nc.vector.tensor_copy(woven[:, cols, 2:].rearrange("p (c i) t -> p c t i", i=4), src.rearrange("p (c i) t -> p c t i", i=4))

        def quantize(i):
            cols = slice(i * PIECE, (i + 1) * PIECE)
            nc.vector.quantize_mx(out=z_codes[:, cols].bitcast(FP8X4), scales=z_scale[:, cols], in_=grouped[:, PACK * cols.start : PACK * cols.stop])

        def quantize_w2(lo, hi):
            nc.vector.quantize_mx(out=w2_codes[:, lo:hi].bitcast(FP8X4), scales=w2_scale[:, lo:hi], in_=w2_grouped[:, PACK * lo : PACK * hi])

        def empty(copy, g, first, end):
            cols = slice(first * PIECE, end * PIECE)
            bank = psum.tile([P, BANK], F32, name="bank")[:, : (end - first) * PIECE]
            for lo, hi in ((first, end),) if end - first != 3 else ((first, first + 2), (first + 2, end)):
                part = bank[:, (lo - first) * PIECE : (hi - first) * PIECE]
                multiply(part, w2_codes, w2_scale, slice(g * P, (g + 1) * P), z_codes, z_scale, slice(lo * PIECE, hi * PIECE))
            copy(results[g][:, cols], bank)

        def store(g, first, end):
            cols = slice(first * PIECE, end * PIECE)
            nc.sync.dma_start(out_rows[:, g, cols], results[g][:, cols])

        scalar, vector = nc.scalar.copy, nc.vector.tensor_copy
        nc.vector.tensor_copy(first_reads.bitcast(U32), page[3][:].bitcast(U32).indirect(entries(rd_sb, 0, PIECE)))
        for first, end in ((1, 3), (3, 5), (5, 8)):
            gather(3, first * PIECE, end * PIECE)
        quantize_w2(0, N // 2)
        nc.vector.tensor_copy(woven[:, :PIECE, 3], first_reads.bitcast(F32))
        quantize_w2(N // 2, N)

        cuts = [(0, 1, 2 + g // 2, 4 + max(0, g - 1), PIECES) for g in range(PACK)]
        last = PIECES - 1
        for i in range(PIECES):
            for ahead in {0: (), 1: (1, 2), last: ()}.get(i, (i + 1,)):
                weave(ahead)
            quantize(i)
            for g in range(PACK):
                if i < last and i + 1 in cuts[g]:
                    first = cuts[g][cuts[g].index(i + 1) - 1]
                    empty(scalar, g, first, i + 1)
                    store(g, first, i + 1)
        empty(scalar, 0, last, PIECES)
        empty(vector, 0, cuts[0][-2], last)
        store(0, cuts[0][-2], PIECES)
        for g in range(1, PACK):
            empty((scalar, vector)[g % 2], g, cuts[g][-2], PIECES)
            store(g, cuts[g][-2], PIECES)
